import numpy as np
import ml_dtypes


def mxq(x, axis, fmt="e4m3"):
    dtype, down = {"e4m3": (ml_dtypes.float8_e4m3fn, 7), "e5m2": (ml_dtypes.float8_e5m2, 14)}[fmt]
    v = np.moveaxis(np.asarray(x, np.float32).astype(ml_dtypes.bfloat16).astype(np.float64), axis, -1)
    blocks = v.reshape(v.shape[:-1] + (-1, 32))
    amax = np.abs(blocks).max(-1, keepdims=True)
    byte = np.maximum(np.where(amax > 0, np.frexp(amax)[1] - 1 + 127, 0) - down, 1)
    scale = np.exp2(byte - 127.0)
    codes = (blocks / scale).astype(np.float32).astype(dtype).astype(np.float64)
    return np.moveaxis((codes * scale).reshape(v.shape), -1, axis)


WIDE = False


def mx_kscale(k):
    if not WIDE:
        return np.ones(k)
    levels = np.array([10, -10, 5, -5, 0])
    if k % 512:
        return np.exp2(np.random.permutation(np.resize(levels, k // 32))).repeat(32)
    a = np.empty((k // 512, 16))
    for p in range(k // 512):
        a[p, :8] = np.random.permutation(np.resize(levels, 8))
        for g in range(8):
            far = levels[np.abs(levels - a[p, g]) >= 10]
            a[p, g + 8] = far[np.random.randint(len(far))]
    return np.exp2(a.ravel()).repeat(32)


def f64(x):
    return np.asarray(x).astype(np.float64)


def striped(idx):
    return np.tile(idx.reshape(-1, 16).T, (8, 1)).astype(np.uint16)


def unstriped(offs):
    return offs[:16].T.reshape(-1).astype(np.int64)


E2M1 = np.array([0.0, 0.5, 1.0, 1.5, 2.0, 3.0, 4.0, 6.0, -0.0, -0.5, -1.0, -1.5, -2.0, -3.0, -4.0, -6.0])


def pack_weight(w, fmt):
    k, n = w.shape
    w = f64(np.asarray(w, np.float32).astype(ml_dtypes.bfloat16)).reshape(k // 32, 32, n)
    amax = np.abs(w).max(1)
    if fmt == "e4m3":
        byte = np.frexp(amax)[1] - 1 + 127 - 7
    else:
        mant, ex = np.frexp(amax / 6.0)
        byte = np.where(mant > 0.5, ex, ex - 1) + 127
    byte = np.clip(np.where(amax > 0, byte, 1), 1, 254)
    scaled = (w * np.exp2(127.0 - byte)[:, None, :]).reshape(k, n).astype(np.float32)
    by_word = np.ascontiguousarray(scaled.reshape(k // 512, 128, 4, n).transpose(0, 1, 3, 2))
    if fmt == "e4m3":
        words = by_word.astype(ml_dtypes.float8_e4m3fn).view(np.uint8)
    else:
        c = by_word.astype(ml_dtypes.float4_e2m1fn).view(np.uint8) & 0xF
        words = (c[..., 0::2] | (c[..., 1::2] << 4)).reshape(k // 512, 128, 2 * n)
    return np.ascontiguousarray(words), np.ascontiguousarray(byte.astype(np.uint8).reshape(k // 512, 16, n))


def unpack_weight(words, scales, fmt):
    g, _, n = scales.shape
    words = np.ascontiguousarray(words).reshape(g, 128, n, -1)
    if fmt == "e4m3":
        vals = words.view(ml_dtypes.float8_e4m3fn).astype(np.float64)
    else:
        nib = np.empty((g, 128, n, 4), np.uint8)
        nib[..., 0::2] = words & 0xF
        nib[..., 1::2] = words >> 4
        vals = E2M1[nib]
    vals = vals * np.repeat(np.exp2(scales.astype(np.float64) - 127.0), 8, axis=1)[..., None]
    return vals.transpose(0, 1, 3, 2).reshape(g * 512, n)


def gelu(v):
    return 0.5 * v * (1.0 + np.tanh(np.sqrt(2.0 / np.pi) * (v + 0.044715 * v**3)))


K, H, N, T, S, T2, P = 1024, 1024, 512, 2048, 1024, 2048, 1024

def setup_inputs():
    n = np.random.standard_normal
    s = mx_kscale(K)[:, None]
    u = mx_kscale(H)[:, None]
    tab_words, tab_scales = pack_weight(n((K, T)) * s, "e4m3")
    w1 = n((K, H)) / np.sqrt(K) / s * u.T
    w2_words, w2_scales = pack_weight(n((H, N)) / np.sqrt(H) / u, "e2m1")
    w3 = n((H, N)) / np.sqrt(H) / u
    return {
        "tab_words": tab_words, "tab_scales": tab_scales,
        "offs": striped(np.random.permutation(T)[:S]),
        "w1": w1.astype(np.float32),
        "wgs": np.exp(0.3 * n((128, S))).astype(np.float32),
        "page0": (n((H, T2)) * u).astype(np.float32),
        "offs2": striped(np.random.permutation(T2)[:S]),
        "offs3": striped(np.random.permutation(T2)[:P]),
        "offs4": striped(np.random.permutation(T2)[:P]),
        "lam": np.random.uniform(0.2, 0.8, H).astype(np.float32),
        "w2_words": w2_words, "w2_scales": w2_scales,
        "w3": w3.astype(np.float32),
    }

def reference(tab_words, tab_scales, offs, w1, wgs, page0, offs2, offs3, offs4, lam, w2_words, w2_scales, w3):
    v = unpack_weight(tab_words, tab_scales, "e4m3")[:, unstriped(offs)]
    h = mxq(f64(w1), 0, "e4m3").T @ v
    page = f64(page0).copy()
    page[:, unstriped(offs2)] = np.tile(f64(wgs), (H // 128, 1)) * h
    x1 = page[:, unstriped(offs3)]
    x2 = page[:, unstriped(offs4)]
    z = mxq(x1 + f64(lam)[:, None] * (x2 - x1), 0, "e4m3")
    num = unpack_weight(w2_words, w2_scales, "e2m1").T @ z
    den = mxq(f64(w3), 0, "e4m3").T @ z
    return num / (1.0 + np.abs(den))

@@ -1,0 +1,325 @@
+from contextlib import ExitStack
+
+import concourse.mybir as mybir
+from concourse.masks import make_identity
+
+K, H, N, T, S, T2, PM = 1024, 1024, 512, 2048, 1024, 2048, 1024
+FLOPS = 2 * K * H * S + 2 * 2 * H * N * PM
+
+F32 = mybir.dt.float32
+BF16 = mybir.dt.bfloat16
+I32 = mybir.dt.int32
+U32 = mybir.dt.uint32
+U16 = mybir.dt.uint16
+U8 = mybir.dt.uint8
+FP8X4 = mybir.dt.float8_e4m3fn_x4
+FP4X4 = mybir.dt.float4_e2m1fn_x4
+ACT = mybir.ActivationFunctionType
+MULT = mybir.AluOpType.mult
+
+P = 128
+PACK = 4
+K_PASS = P * PACK
+PASSES = 2
+BANK = 512
+ROW_TILES = H // P
+HALF = S // 2
+W1_CHUNKS = [(0, 128), (128, 256), (256, 512), (512, 768), (768, 1024)]
+CHUNKS = [(0, 256), (256, 512), (512, 768), (768, 1024)]
+H_BUFS = 8
+X_SLOTS = 2
+
+
+def tile_list_hive_diary_kernel(
+    tc, tab_words, tab_scales, offs, w1, wgs, page0, offs2, offs3, offs4, lam, w2_words, w2_scales, w3, out
+):
+    nc = tc.nc
+    with ExitStack() as ctx:
+        keep = ctx.enter_context(tc.tile_pool(name="keep", bufs=1))
+        stage = ctx.enter_context(tc.tile_pool(name="stage", bufs=2))
+        psum = ctx.enter_context(tc.psum_pool(name="psum", bufs=1))
+
+        def held(name, shape, dtype):
+            return keep.tile(shape, dtype, name=name, align_bytes=64)
+
+        lists = [keep.tile([P, S // 16], U16, name=f"list{n}") for n in range(4)]
+        tab_list, put_list, before_list, after_list = lists
+        words = [held(f"words{a}", [P, T], U32) for a in range(PASSES)]
+        planes = held("planes", [P, T], U8)
+        picked_words = [[held(f"pw{a}_{hf}", [P, HALF], U32) for hf in range(2)] for a in range(PASSES)]
+        picked_planes = [held(f"pp{hf}", [P, HALF], U8) for hf in range(2)]
+        pages = [held(f"page{i}", [P, T2], F32) for i in range(ROW_TILES)]
+        wgs_sb = held("wgs_sb", [P, S], F32)
+        lam_rows = held("lam_rows", [P, P], F32)
+        lam_cols = held("lam_cols", [P, ROW_TILES], F32)
+        rest_cols = held("rest_cols", [P, ROW_TILES], F32)
+        one = held("one", [P, 1], F32)
+        ident = held("ident", [P, P], F32)
+        w2_codes = held("w2_codes", [P, PASSES, 2 * N], U8)
+        w2_planes = held("w2_planes", [P, PASSES, N], U8)
+        h_bufs = [held(f"h{n}", [P, S], F32) for n in range(H_BUFS)]
+        banks = [psum.tile([P, BANK], F32, name=f"bank{b}") for b in range(8)]
+        h_banks, sum_banks, word_banks = banks[0:2], banks[2:4], banks[4:6]
+        den_banks, num_banks = [banks[6], banks[0]], [banks[7], banks[1]]
+
+        def load_weight(name, w, c0, c1):
+            raws = []
+            for a in range(PASSES):
+                raw = stage.tile([P, PACK, c1 - c0], F32, name=f"{name}_raw{a}_{c0}", tag="raw", bufs=6)
+                rows = w[a * K_PASS : (a + 1) * K_PASS, c0:c1].rearrange("(p j) c -> p j c", j=PACK)
+                nc.sync.dma_start(out=raw[:], in_=rows)
+                raws.append(raw)
+            return raws
+
+        def quantize_weight(name, raws):
+            width = raws[0].shape[2]
+            grouped = stage.tile([P, PASSES, width, PACK], BF16, name="grouped", tag="grouped", bufs=3, align_bytes=64)
+            for a in range(PASSES):
+                nc.scalar.copy(
+                    out=grouped[:, a, :, :].rearrange("p (c i) j -> p c j i", i=4),
+                    in_=raws[a][:].rearrange("p j (c i) -> p c j i", i=4),
+                )
+            codes = held(f"{name}_codes", [P, PASSES * width], U32)
+            scales = held(f"{name}_scales", [P, PASSES * width], U8)
+            nc.vector.quantize_mx(
+                out=codes[:].bitcast(FP8X4), scales=scales[:], in_=grouped[:].rearrange("p a c j -> p (a c j)")
+            )
+            return codes, scales, width
+
+        def load_page(i):
+            nc.sync.dma_start(out=pages[i][:], in_=page0[i * P : (i + 1) * P, :])
+
+        nc.gpsimd.memset(planes[:].bitcast(I32), 0)
+        nc.gpsimd.memset(one[:], 1.0)
+        nc.sync.dma_start(tab_list[:], offs)
+        for q in range(4):
+            nc.sync.dma_start(
+                out=planes[32 * q : 32 * q + 4 * PASSES, :].bitcast(I32),
+                in_=tab_scales[:, 4 * q : 4 * q + 4, :].bitcast(I32),
+            )
+        nc.sync.dma_start(out=words[0][:].bitcast(I32), in_=tab_words[0].rearrange("p t i -> p (t i)").bitcast(I32))
+        w1_raw = [load_weight("w1", w1, *W1_CHUNKS[0])]
+        nc.sync.dma_start(out=words[1][:].bitcast(I32), in_=tab_words[1].rearrange("p t i -> p (t i)").bitcast(I32))
+        nc.sync.dma_start(out=wgs_sb[:, 0:HALF], in_=wgs[:, 0:HALF])
+        w1_raw.append(load_weight("w1", w1, *W1_CHUNKS[1]))
+        nc.sync.dma_start(put_list[:], offs2)
+        load_page(0)
+        nc.sync.dma_start(out=wgs_sb[:, HALF:S], in_=wgs[:, HALF:S])
+        for c in range(2, len(W1_CHUNKS)):
+            w1_raw.append(load_weight("w1", w1, *W1_CHUNKS[c]))
+            if c == 2:
+                nc.sync.dma_start(out=w2_codes[:].bitcast(I32), in_=w2_words.rearrange("a p c -> p a c").bitcast(I32))
+            load_page(c - 1)
+        w3_raw = []
+        for c in range(2):
+            w3_raw.append(load_weight("w3", w3, c * N // 2, (c + 1) * N // 2))
+            load_page(4 + c)
+        nc.sync.dma_start(before_list[:], offs3)
+        nc.sync.dma_start(after_list[:], offs4)
+        nc.gpsimd.memset(lam_rows[:], 0.0)
+        nc.sync.dma_start(out=lam_rows[0:ROW_TILES, :], in_=lam.rearrange("(i p) -> i p", p=P))
+        load_page(6)
+        load_page(7)
+        nc.gpsimd.memset(w2_planes[:].bitcast(I32), 0)
+        for q in range(4):
+            nc.sync.dma_start(
+                out=w2_planes[32 * q : 32 * q + 4, :, :].bitcast(I32),
+                in_=w2_scales[:, 4 * q : 4 * q + 4, :].rearrange("a r c -> r a c").bitcast(I32),
+            )
+        make_identity(nc, ident[:])
+
+        def pick_words(a, hf):
+            cols = tab_list[:, hf * HALF // 16 : (hf + 1) * HALF // 16]
+            nc.vector.tensor_copy(picked_words[a][hf][:], words[a][:].indirect(cols))
+
+        def pick_planes(hf):
+            cols = tab_list[:, hf * HALF // 16 : (hf + 1) * HALF // 16]
+            nc.vector.tensor_copy(picked_planes[hf][:], planes[:].indirect(cols))
+
+        pick_planes(0)
+        pick_words(0, 0)
+        w1_mx = [quantize_weight("w1_0", w1_raw[0])]
+        pick_words(1, 0)
+        pick_planes(1)
+        pick_words(0, 1)
+        pick_words(1, 1)
+
+
+        def write_entries(i):
+            c = [n for n, (c0, c1) in enumerate(W1_CHUNKS) if c0 <= i * P < c1][0]
+            codes, scales, width = w1_mx[c]
+            first = i * P - W1_CHUNKS[c][0]
+            h = h_bufs[i % H_BUFS]
+            for hf in range(2):
+                for a in range(PASSES):
+                    cols = slice(a * width + first, a * width + first + P)
+                    nc.tensor.matmul_mx(
+                        out=h_banks[hf][:],
+                        lhsT=codes[:, cols].bitcast(FP8X4),
+                        lhsT_scale=scales[:, cols],
+                        rhs=picked_words[a][hf][:].bitcast(FP8X4),
+                        rhs_scale=picked_planes[hf][4 * a : P, :],
+                        start=(a == 0),
+                        stop=(a == PASSES - 1),
+                    )
+                nc.scalar.copy(out=h[:, hf * HALF : (hf + 1) * HALF], in_=h_banks[hf][:])
+            pieces = [(0, HALF), (HALF, S)] if i == 0 else [(0, S)]
+            for j0, j1 in pieces:
+                nc.vector.tensor_tensor(
+                    pages[i][:].indirect(put_list[:, j0 // 16 : j1 // 16]), h[:, j0:j1], wgs_sb[:, j0:j1], MULT
+                )
+
+        z_ring = [held(f"zt{n}", [P, 2, 2, P, 2], BF16) for n in range(3)]
+        z_t = [[z_ring[(c * PASSES + b) % 3] for b in range(PASSES)] for c in range(len(CHUNKS))]
+        z_codes = [[held(f"zc{c}_{b}", [P, m1 - m0], U32) for b in range(PASSES)] for c, (m0, m1) in enumerate(CHUNKS)]
+        z_scales = [[held(f"zs{c}_{b}", [P, m1 - m0], U8) for b in range(PASSES)] for c, (m0, m1) in enumerate(CHUNKS)]
+        scaled = [held(f"scaled{n}", [P, 2 * 256], F32) for n in range(2)]
+        freed = [h_bufs[(ROW_TILES - 1) % H_BUFS], wgs_sb]
+        late_x = [freed[n // 2][:, (n % 2) * HALF : (n % 2 + 1) * HALF] for n in range(X_SLOTS)]
+
+        def fetch(c, i):
+            m0, m1 = CHUNKS[c]
+            width = m1 - m0
+            x = late_x[(c * ROW_TILES + i) % X_SLOTS]
+            y = scaled[(c * ROW_TILES + i) % 2]
+            for n, (visits, weight) in enumerate(((before_list, rest_cols), (after_list, lam_cols))):
+                cols = slice(n * width, (n + 1) * width)
+                nc.vector.tensor_copy(x[:, cols], pages[i][:].indirect(visits[:, m0 // 16 : m1 // 16]))
+                nc.scalar.activation(out=y[:, cols], in_=x[:, cols], func=ACT.Copy, scale=weight[:, i : i + 1])
+            bank = sum_banks[i % 2]
+            for j in range(width // P):
+                for n in range(2):
+                    nc.tensor.matmul(
+                        bank[:, j * P : (j + 1) * P],
+                        y[:, n * width + j * P : n * width + (j + 1) * P],
+                        ident[:],
+                        is_transpose=True,
+                        start=(n == 0),
+                        stop=(n == 1),
+                    )
+            quarter = i % PACK
+            nc.scalar.copy(
+                out=z_t[c][i // PACK][:, :, :, 32 * quarter : 32 * (quarter + 1), :],
+                in_=bank[:, 0:width].rearrange("m (j p u e) -> m u j p e", p=32, u=2, e=2),
+            )
+
+        def quantize_z(c, b):
+            m0, m1 = CHUNKS[c]
+            blocks = (m1 - m0) // P
+            pairs = z_t[c][b][:].rearrange("m u j p e -> m (u j p e)").bitcast(F32)
+            grouped = stage.tile([P, (m1 - m0) * PACK], BF16, name="z_grouped", tag="z_grouped", align_bytes=64)
+            for j0 in range(0, blocks, 2):
+                bank = word_banks[(b + j0 // 2) % 2]
+                for jj in range(2):
+                    for u in range(2):
+                        src = (u * blocks + j0 + jj) * P
+                        dst = (jj * 2 + u) * P
+                        nc.tensor.transpose(bank[:, dst : dst + P], pairs[:, src : src + P], ident[:])
+                nc.scalar.copy(
+                    out=grouped[:].bitcast(F32)[:, j0 * 2 * P : (j0 + 2) * 2 * P].rearrange("p (j m u) -> p j m u", j=2, u=2),
+                    in_=bank[:].rearrange("p (j u m) -> p j m u", j=2, u=2),
+                )
+            nc.vector.quantize_mx(out=z_codes[c][b][:].bitcast(FP8X4), scales=z_scales[c][b][:], in_=grouped[:])
+
+        def den_sums(c, nt, bank, first):
+            width = CHUNKS[c][1] - CHUNKS[c][0]
+            codes, scales, w3_width = w3_mx[nt // 2]
+            for b in range(PASSES):
+                cols = slice(b * w3_width + (nt % 2) * P, b * w3_width + (nt % 2 + 1) * P)
+                nc.tensor.matmul_mx(
+                    out=bank[:, first : first + width],
+                    lhsT=codes[:, cols].bitcast(FP8X4),
+                    lhsT_scale=scales[:, cols],
+                    rhs=z_codes[c][b][:].bitcast(FP8X4),
+                    rhs_scale=z_scales[c][b][:],
+                    start=(b == 0),
+                    stop=(b == PASSES - 1),
+                )
+
+        def num_sums(c, nt, bank, first):
+            width = CHUNKS[c][1] - CHUNKS[c][0]
+            for g0 in range(0, width, P):
+                for b in range(PASSES):
+                    nc.tensor.matmul_mx(
+                        out=bank[:, first + g0 : first + g0 + P],
+                        lhsT=w2_codes[:, b, 2 * nt * P : 2 * (nt + 1) * P].bitcast(FP4X4),
+                        lhsT_scale=w2_planes[:, b, nt * P : (nt + 1) * P],
+                        rhs=z_codes[c][b][:, g0 : g0 + P].bitcast(FP8X4),
+                        rhs_scale=z_scales[c][b][:, g0 : g0 + P],
+                        start=(b == 0),
+                        stop=(b == PASSES - 1),
+                    )
+
+        def score_steps(c, pair):
+            m0, m1 = CHUNKS[c]
+            width = m1 - m0
+            den, num = den_banks[pair], num_banks[pair]
+            size = stage.tile([P, BANK], F32, name="size", tag="size")
+            root = stage.tile([P, BANK], F32, name="root", tag="root")
+            inverse = stage.tile([P, BANK], F32, name="inverse", tag="inverse")
+            result = stage.tile([P, BANK], F32, name="result", tag="result")
+
+            def sums():
+                for half in range(2):
+                    den_sums(c, 2 * pair + half, den, half * width)
+                for half in range(2):
+                    num_sums(c, 2 * pair + half, num, half * width)
+                nc.scalar.activation(out=size[:], in_=den[:], func=ACT.Abs)
+
+            def inverse_root():
+                nc.scalar.activation(out=root[:], in_=size[:], func=ACT.Abs_reciprocal_sqrt, bias=one[:])
+
+            def finish():
+                nc.scalar.activation(out=inverse[:], in_=root[:], func=ACT.Square)
+                nc.vector.tensor_tensor(result[:], num[:], inverse[:], MULT)
+                nc.sync.dma_start(
+                    out=out[2 * pair * P : 2 * (pair + 1) * P, m0:m1].rearrange("(t p) m -> p t m", p=P),
+                    in_=result[:].rearrange("p (t m) -> p t m", t=2),
+                )
+
+            return [sums, inverse_root, finish]
+
+        w3_mx = []
+        for i in range(ROW_TILES):
+            if i + 1 < len(W1_CHUNKS):
+                w1_mx.append(quantize_weight(f"w1_{i + 1}", w1_raw[i + 1]))
+            elif len(w3_mx) < 2:
+                w3_mx.append(quantize_weight(f"w3_{i}", w3_raw[len(w3_mx)]))
+            write_entries(i)
+        nc.tensor.transpose(h_banks[1][:, 0:P], lam_rows[:], ident[:])
+        nc.scalar.copy(out=lam_cols[:], in_=h_banks[1][:, 0:ROW_TILES])
+        nc.scalar.activation(out=rest_cols[:], in_=h_banks[1][:, 0:ROW_TILES], func=ACT.Copy, scale=-1.0, bias=1.0)
+        waiting = []
+        for c in range(len(CHUNKS)):
+            for i in range(ROW_TILES):
+                fetch(c, i)
+                if i % PACK == PACK - 1:
+                    quantize_z(c, i // PACK)
+                    if i == PACK - 1 and c > 0:
+                        waiting = waiting + score_steps(c - 1, 0) + score_steps(c - 1, 1)
+                elif waiting and not (c == len(CHUNKS) - 1 and i >= PACK):
+                    waiting[0]()
+                    waiting = waiting[1:]
+        for step in waiting:
+            step()
+        c = len(CHUNKS) - 1
+        m0, m1 = CHUNKS[c]
+        width = m1 - m0
+        tail_den = [banks[2], banks[3], banks[6], banks[0]]
+        tail_num = [banks[4], banks[5], banks[7], banks[1]]
+        roots = []
+        for nt in range(N // P):
+            den_sums(c, nt, tail_den[nt], 0)
+        for nt in range(N // P):
+            num_sums(c, nt, tail_num[nt], 0)
+        for nt in range(N // P):
+            size = held(f"tail_size{nt}", [P, width], F32)
+            nc.scalar.activation(out=size[:], in_=tail_den[nt][:, 0:width], func=ACT.Abs)
+            roots.append(size)
+        for nt in range(N // P):
+            root = held(f"tail_root{nt}", [P, width], F32)
+            once = held(f"tail_once{nt}", [P, width], F32)
+            nc.scalar.activation(out=root[:], in_=roots[nt][:], func=ACT.Abs_reciprocal_sqrt, bias=one[:])
+            nc.vector.tensor_tensor(once[:], tail_num[nt][:, 0:width], root[:], MULT)
+            nc.vector.tensor_tensor(roots[nt][:], once[:], root[:], MULT)
+            nc.sync.dma_start(out=out[nt * P : (nt + 1) * P, m0:m1], in_=roots[nt][:])

@@ -25,9 +25,13 @@ BANK = 512
 ROW_TILES = H // P
 HALF = S // 2
 W1_CHUNKS = [(0, 128), (128, 256), (256, 512), (512, 768), (768, 1024)]
-CHUNKS = [(0, 256), (256, 512), (512, 768), (768, 1024)]
+CHUNKS = [(0, 512), (512, 768), (768, 1024)]
 H_BUFS = 8
 X_SLOTS = 2
+LAG = 2
+NS = 3
+QL = 1
+ST = 6
 
 
 def tile_list_hive_diary_kernel(
@@ -59,7 +63,7 @@ def tile_list_hive_diary_kernel(
         w2_planes = held("w2_planes", [P, PASSES, N], U8)
         h_bufs = [held(f"h{n}", [P, S], F32) for n in range(H_BUFS)]
         banks = [psum.tile([P, BANK], F32, name=f"bank{b}") for b in range(8)]
-        h_banks, sum_banks, word_banks = banks[0:2], banks[2:4], banks[4:6]
+        h_banks, sum_banks, word_banks = banks[0:2], banks[2:2+NS], banks[2+NS:6]
         den_banks, num_banks = [banks[6], banks[0]], [banks[7], banks[1]]
 
         def load_weight(name, w, c0, c1):
@@ -91,6 +95,8 @@ def tile_list_hive_diary_kernel(
 
         nc.gpsimd.memset(planes[:].bitcast(I32), 0)
         nc.gpsimd.memset(one[:], 1.0)
+        warm = held("warm", [P, 1], F32)
+        nc.scalar.activation(out=warm[:], in_=one[:], func=ACT.Abs_reciprocal_sqrt, bias=one[:])
         nc.sync.dma_start(tab_list[:], offs)
         for q in range(4):
             nc.sync.dma_start(
@@ -163,53 +169,65 @@ def tile_list_hive_diary_kernel(
                         stop=(a == PASSES - 1),
                     )
                 nc.scalar.copy(out=h[:, hf * HALF : (hf + 1) * HALF], in_=h_banks[hf][:])
+
+        def put(i):
+            h = h_bufs[i % H_BUFS]
             pieces = [(0, HALF), (HALF, S)] if i == 0 else [(0, S)]
             for j0, j1 in pieces:
                 nc.vector.tensor_tensor(
                     pages[i][:].indirect(put_list[:, j0 // 16 : j1 // 16]), h[:, j0:j1], wgs_sb[:, j0:j1], MULT
                 )
 
-        z_ring = [held(f"zt{n}", [P, 2, 2, P, 2], BF16) for n in range(3)]
-        z_t = [[z_ring[(c * PASSES + b) % 3] for b in range(PASSES)] for c in range(len(CHUNKS))]
+        z_ring = [held(f"zt{n}", [P, PACK * BANK], BF16) for n in range(2)]
         z_codes = [[held(f"zc{c}_{b}", [P, m1 - m0], U32) for b in range(PASSES)] for c, (m0, m1) in enumerate(CHUNKS)]
         z_scales = [[held(f"zs{c}_{b}", [P, m1 - m0], U8) for b in range(PASSES)] for c, (m0, m1) in enumerate(CHUNKS)]
-        scaled = [held(f"scaled{n}", [P, 2 * 256], F32) for n in range(2)]
-        freed = [h_bufs[(ROW_TILES - 1) % H_BUFS], wgs_sb]
-        late_x = [freed[n // 2][:, (n % 2) * HALF : (n % 2 + 1) * HALF] for n in range(X_SLOTS)]
+        scaled = h_bufs[0:NS]
+        late_x = [h_bufs[ROW_TILES - 1], wgs_sb, h_bufs[ROW_TILES - 2]]
+
+        def z_t(c, b):
+            width = CHUNKS[c][1] - CHUNKS[c][0]
+            return z_ring[b][:, 0 : PACK * width]
 
         def fetch(c, i):
             m0, m1 = CHUNKS[c]
             width = m1 - m0
-            x = late_x[(c * ROW_TILES + i) % X_SLOTS]
-            y = scaled[(c * ROW_TILES + i) % 2]
+            turn = c * ROW_TILES + i
+            x = late_x[turn % X_SLOTS]
+            y = scaled[turn % NS]
+            bank = sum_banks[turn % NS]
             for n, (visits, weight) in enumerate(((before_list, rest_cols), (after_list, lam_cols))):
                 cols = slice(n * width, (n + 1) * width)
                 nc.vector.tensor_copy(x[:, cols], pages[i][:].indirect(visits[:, m0 // 16 : m1 // 16]))
                 nc.scalar.activation(out=y[:, cols], in_=x[:, cols], func=ACT.Copy, scale=weight[:, i : i + 1])
-            bank = sum_banks[i % 2]
             for j in range(width // P):
-                for n in range(2):
+                for n in (1, 0):
                     nc.tensor.matmul(
                         bank[:, j * P : (j + 1) * P],
                         y[:, n * width + j * P : n * width + (j + 1) * P],
                         ident[:],
                         is_transpose=True,
-                        start=(n == 0),
-                        stop=(n == 1),
+                        start=(n == 1),
+                        stop=(n == 0),
                     )
+
+        def collect(c, i):
+            width = CHUNKS[c][1] - CHUNKS[c][0]
+            bank = sum_banks[(c * ROW_TILES + i) % NS]
             quarter = i % PACK
             nc.scalar.copy(
-                out=z_t[c][i // PACK][:, :, :, 32 * quarter : 32 * (quarter + 1), :],
+                out=z_t(c, i // PACK).rearrange("m (u j p e) -> m u j p e", u=2, p=P, e=2)[
+                    :, :, :, 32 * quarter : 32 * (quarter + 1), :
+                ],
                 in_=bank[:, 0:width].rearrange("m (j p u e) -> m u j p e", p=32, u=2, e=2),
             )
 
         def quantize_z(c, b):
             m0, m1 = CHUNKS[c]
             blocks = (m1 - m0) // P
-            pairs = z_t[c][b][:].rearrange("m u j p e -> m (u j p e)").bitcast(F32)
+            pairs = z_t(c, b).bitcast(F32)
             grouped = stage.tile([P, (m1 - m0) * PACK], BF16, name="z_grouped", tag="z_grouped", align_bytes=64)
             for j0 in range(0, blocks, 2):
-                bank = word_banks[(b + j0 // 2) % 2]
+                bank = word_banks[(b + j0 // 2) % len(word_banks)]
                 for jj in range(2):
                     for u in range(2):
                         src = (u * blocks + j0 + jj) * P
@@ -238,43 +256,42 @@ def tile_list_hive_diary_kernel(
 
         def num_sums(c, nt, bank, first):
             width = CHUNKS[c][1] - CHUNKS[c][0]
-            for g0 in range(0, width, P):
+            step = BANK if width == BANK else P
+            for g0 in range(0, width, step):
                 for b in range(PASSES):
                     nc.tensor.matmul_mx(
-                        out=bank[:, first + g0 : first + g0 + P],
+                        out=bank[:, first + g0 : first + g0 + step],
                         lhsT=w2_codes[:, b, 2 * nt * P : 2 * (nt + 1) * P].bitcast(FP4X4),
                         lhsT_scale=w2_planes[:, b, nt * P : (nt + 1) * P],
-                        rhs=z_codes[c][b][:, g0 : g0 + P].bitcast(FP8X4),
-                        rhs_scale=z_scales[c][b][:, g0 : g0 + P],
+                        rhs=z_codes[c][b][:, g0 : g0 + step].bitcast(FP8X4),
+                        rhs_scale=z_scales[c][b][:, g0 : g0 + step],
                         start=(b == 0),
                         stop=(b == PASSES - 1),
                     )
 
-        def score_steps(c, pair):
+        def score_steps(u, c, tiles, den, num):
             m0, m1 = CHUNKS[c]
             width = m1 - m0
-            den, num = den_banks[pair], num_banks[pair]
-            size = stage.tile([P, BANK], F32, name="size", tag="size")
-            root = stage.tile([P, BANK], F32, name="root", tag="root")
-            inverse = stage.tile([P, BANK], F32, name="inverse", tag="inverse")
-            result = stage.tile([P, BANK], F32, name="result", tag="result")
+            cols = slice(0, len(tiles) * width)
+            size, root, part = [h_bufs[n][:, (u % 2) * BANK : (u % 2 + 1) * BANK] for n in (3, 4, 5)]
+            result = stage.tile([P, BANK], F32, name="result", tag="result", bufs=3)
 
             def sums():
-                for half in range(2):
-                    den_sums(c, 2 * pair + half, den, half * width)
-                for half in range(2):
-                    num_sums(c, 2 * pair + half, num, half * width)
-                nc.scalar.activation(out=size[:], in_=den[:], func=ACT.Abs)
+                for n, nt in enumerate(tiles):
+                    den_sums(c, nt, den, n * width)
+                for n, nt in enumerate(tiles):
+                    num_sums(c, nt, num, n * width)
+                nc.scalar.activation(out=size[:, cols], in_=den[:, cols], func=ACT.Abs)
 
             def inverse_root():
-                nc.scalar.activation(out=root[:], in_=size[:], func=ACT.Abs_reciprocal_sqrt, bias=one[:])
+                nc.scalar.activation(out=root[:, cols], in_=size[:, cols], func=ACT.Abs_reciprocal_sqrt, bias=one[:])
 
             def finish():
-                nc.scalar.activation(out=inverse[:], in_=root[:], func=ACT.Square)
-                nc.vector.tensor_tensor(result[:], num[:], inverse[:], MULT)
+                nc.vector.tensor_tensor(part[:, cols], num[:, cols], root[:, cols], MULT)
+                nc.vector.tensor_tensor(result[:, cols], part[:, cols], root[:, cols], MULT)
                 nc.sync.dma_start(
-                    out=out[2 * pair * P : 2 * (pair + 1) * P, m0:m1].rearrange("(t p) m -> p t m", p=P),
-                    in_=result[:].rearrange("p (t m) -> p t m", t=2),
+                    out=out[tiles[0] * P : (tiles[-1] + 1) * P, m0:m1].rearrange("(t p) m -> p t m", p=P),
+                    in_=result[:, cols].rearrange("p (t m) -> p t m", t=len(tiles)),
                 )
 
             return [sums, inverse_root, finish]
@@ -286,40 +303,40 @@ def tile_list_hive_diary_kernel(
             elif len(w3_mx) < 2:
                 w3_mx.append(quantize_weight(f"w3_{i}", w3_raw[len(w3_mx)]))
             write_entries(i)
+            put(i)
         nc.tensor.transpose(h_banks[1][:, 0:P], lam_rows[:], ident[:])
         nc.scalar.copy(out=lam_cols[:], in_=h_banks[1][:, 0:ROW_TILES])
         nc.scalar.activation(out=rest_cols[:], in_=h_banks[1][:, 0:ROW_TILES], func=ACT.Copy, scale=-1.0, bias=1.0)
-        waiting = []
-        for c in range(len(CHUNKS)):
-            for i in range(ROW_TILES):
-                fetch(c, i)
-                if i % PACK == PACK - 1:
-                    quantize_z(c, i // PACK)
-                    if i == PACK - 1 and c > 0:
-                        waiting = waiting + score_steps(c - 1, 0) + score_steps(c - 1, 1)
-                elif waiting and not (c == len(CHUNKS) - 1 and i >= PACK):
-                    waiting[0]()
-                    waiting = waiting[1:]
-        for step in waiting:
-            step()
-        c = len(CHUNKS) - 1
-        m0, m1 = CHUNKS[c]
-        width = m1 - m0
+        last = len(CHUNKS) - 1
+        units = []
+        for c in range(last):
+            group = BANK // (CHUNKS[c][1] - CHUNKS[c][0])
+            for nt in range(0, N // P, group):
+                units.append((c, list(range(nt, nt + group)), den_banks[len(units) % 2], num_banks[len(units) % 2]))
         tail_den = [banks[2], banks[3], banks[6], banks[0]]
         tail_num = [banks[4], banks[5], banks[7], banks[1]]
-        roots = []
         for nt in range(N // P):
-            den_sums(c, nt, tail_den[nt], 0)
-        for nt in range(N // P):
-            num_sums(c, nt, tail_num[nt], 0)
-        for nt in range(N // P):
-            size = held(f"tail_size{nt}", [P, width], F32)
-            nc.scalar.activation(out=size[:], in_=tail_den[nt][:, 0:width], func=ACT.Abs)
-            roots.append(size)
-        for nt in range(N // P):
-            root = held(f"tail_root{nt}", [P, width], F32)
-            once = held(f"tail_once{nt}", [P, width], F32)
-            nc.scalar.activation(out=root[:], in_=roots[nt][:], func=ACT.Abs_reciprocal_sqrt, bias=one[:])
-            nc.vector.tensor_tensor(once[:], tail_num[nt][:, 0:width], root[:], MULT)
-            nc.vector.tensor_tensor(roots[nt][:], once[:], root[:], MULT)
-            nc.sync.dma_start(out=out[nt * P : (nt + 1) * P, m0:m1], in_=roots[nt][:])
+            units.append((last, [nt], tail_den[nt], tail_num[nt]))
+        waiting = []
+        for n, unit in enumerate(units):
+            steps = score_steps(n, *unit)
+            waiting.append(steps)
+        queue = []
+        for n in range(len(units) + 2):
+            for k in (2, 1, 0):
+                if 0 <= n - k < len(units):
+                    queue.append((units[n - k][0], waiting[n - k][k]))
+        turns = len(CHUNKS) * ROW_TILES
+        for turn in range(turns + LAG + QL):
+            if turn < turns:
+                fetch(*divmod(turn, ROW_TILES))
+            if 0 <= turn - LAG < turns:
+                collect(*divmod(turn - LAG, ROW_TILES))
+            c, i = divmod(turn - LAG - QL, ROW_TILES)
+            if c >= 0 and i % PACK == PACK - 1:
+                quantize_z(c, i // PACK)
+            elif turn >= ROW_TILES + ST and turn < turns and queue[0][0] < len(CHUNKS) - 1:
+                queue[0][1]()
+                queue = queue[1:]
+        for c, step in queue:
+            step()

@@ -24,9 +24,8 @@ PASSES = 2
 BANK = 512
 ROW_TILES = H // P
 HALF = S // 2
-W1_CHUNKS = [(0, 128), (128, 256), (256, 512), (512, 768), (768, 1024)]
+W1_CHUNKS = [(0, 256), (256, 512), (512, 768), (768, 1024)]
 CHUNKS = [(0, 512), (512, 768), (768, 1024)]
-H_BUFS = 8
 X_SLOTS = 2
 LAG = 2
 NS = 3
@@ -61,33 +60,35 @@ def tile_list_hive_diary_kernel(
         ident = held("ident", [P, P], F32)
         w2_codes = held("w2_codes", [P, PASSES, 2 * N], U8)
         w2_planes = held("w2_planes", [P, PASSES, N], U8)
-        h_bufs = [held(f"h{n}", [P, S], F32) for n in range(H_BUFS)]
+        rooms = [held(f"room{c}", [P, PASSES * PACK * (c1 - c0)], F32) for c, (c0, c1) in enumerate(W1_CHUNKS)]
+        casts = [held(f"cast{n}", [P, S], F32) for n in range(2)]
+        low, high = slice(0, S), slice(S, 2 * S)
+        h_bufs = [None, rooms[1][:, high], rooms[0][:, low], rooms[2][:, high], rooms[1][:, low], rooms[3][:, high],
+                  rooms[2][:, low], rooms[0][:, high]]
         banks = [psum.tile([P, BANK], F32, name=f"bank{b}") for b in range(8)]
         h_banks, sum_banks, word_banks = banks[0:2], banks[2:2+NS], banks[2+NS:6]
         den_banks, num_banks = [banks[6], banks[0]], [banks[7], banks[1]]
 
-        def load_weight(name, w, c0, c1):
-            raws = []
+        def load_weight(w, c0, c1, room):
+            size = PACK * (c1 - c0)
+            raws = [room[:, a * size : (a + 1) * size].rearrange("p (j c) -> p j c", j=PACK) for a in range(PASSES)]
             for a in range(PASSES):
-                raw = stage.tile([P, PACK, c1 - c0], F32, name=f"{name}_raw{a}_{c0}", tag="raw", bufs=6)
                 rows = w[a * K_PASS : (a + 1) * K_PASS, c0:c1].rearrange("(p j) c -> p j c", j=PACK)
-                nc.sync.dma_start(out=raw[:], in_=rows)
-                raws.append(raw)
+                nc.sync.dma_start(out=raws[a], in_=rows)
             return raws
 
-        def quantize_weight(name, raws):
+        def quantize_weight(name, raws, cast):
             width = raws[0].shape[2]
-            grouped = stage.tile([P, PASSES, width, PACK], BF16, name="grouped", tag="grouped", bufs=3, align_bytes=64)
+            values = PASSES * PACK * width
+            grouped = cast[:].bitcast(BF16)[:, 2 * S - values : 2 * S]
             for a in range(PASSES):
                 nc.scalar.copy(
-                    out=grouped[:, a, :, :].rearrange("p (c i) j -> p c j i", i=4),
-                    in_=raws[a][:].rearrange("p j (c i) -> p c j i", i=4),
+                    out=grouped[:, a * PACK * width : (a + 1) * PACK * width].rearrange("p (c i j) -> p c j i", i=4, j=PACK),
+                    in_=raws[a].rearrange("p j (c i) -> p c j i", i=4),
                 )
             codes = held(f"{name}_codes", [P, PASSES * width], U32)
             scales = held(f"{name}_scales", [P, PASSES * width], U8)
-            nc.vector.quantize_mx(
-                out=codes[:].bitcast(FP8X4), scales=scales[:], in_=grouped[:].rearrange("p a c j -> p (a c j)")
-            )
+            nc.vector.quantize_mx(out=codes[:].bitcast(FP8X4), scales=scales[:], in_=grouped)
             return codes, scales, width
 
         def load_page(i):
@@ -104,22 +105,17 @@ def tile_list_hive_diary_kernel(
                 in_=tab_scales[:, 4 * q : 4 * q + 4, :].bitcast(I32),
             )
         nc.sync.dma_start(out=words[0][:].bitcast(I32), in_=tab_words[0].rearrange("p t i -> p (t i)").bitcast(I32))
-        w1_raw = [load_weight("w1", w1, *W1_CHUNKS[0])]
+        w1_raw = [load_weight(w1, *W1_CHUNKS[0], rooms[0])]
         nc.sync.dma_start(out=words[1][:].bitcast(I32), in_=tab_words[1].rearrange("p t i -> p (t i)").bitcast(I32))
-        nc.sync.dma_start(out=wgs_sb[:, 0:HALF], in_=wgs[:, 0:HALF])
-        w1_raw.append(load_weight("w1", w1, *W1_CHUNKS[1]))
+        nc.sync.dma_start(out=wgs_sb[:], in_=wgs)
         nc.sync.dma_start(put_list[:], offs2)
         load_page(0)
-        nc.sync.dma_start(out=wgs_sb[:, HALF:S], in_=wgs[:, HALF:S])
-        for c in range(2, len(W1_CHUNKS)):
-            w1_raw.append(load_weight("w1", w1, *W1_CHUNKS[c]))
-            if c == 2:
-                nc.sync.dma_start(out=w2_codes[:].bitcast(I32), in_=w2_words.rearrange("a p c -> p a c").bitcast(I32))
-            load_page(c - 1)
-        w3_raw = []
-        for c in range(2):
-            w3_raw.append(load_weight("w3", w3, c * N // 2, (c + 1) * N // 2))
-            load_page(4 + c)
+        for c in range(1, len(W1_CHUNKS)):
+            w1_raw.append(load_weight(w1, *W1_CHUNKS[c], rooms[c]))
+            load_page(c)
+        load_page(4)
+        load_page(5)
+        nc.sync.dma_start(out=w2_codes[:].bitcast(I32), in_=w2_words.rearrange("a p c -> p a c").bitcast(I32))
         nc.sync.dma_start(before_list[:], offs3)
         nc.sync.dma_start(after_list[:], offs4)
         nc.gpsimd.memset(lam_rows[:], 0.0)
@@ -144,18 +140,20 @@ def tile_list_hive_diary_kernel(
 
         pick_planes(0)
         pick_words(0, 0)
-        w1_mx = [quantize_weight("w1_0", w1_raw[0])]
         pick_words(1, 0)
+        w1_mx = [quantize_weight("w1_0", w1_raw[0], casts[0])]
         pick_planes(1)
         pick_words(0, 1)
         pick_words(1, 1)
 
 
+        def h_half(i, hf):
+            return casts[1 - hf][:, HALF // 2 : HALF // 2 + HALF] if i == 0 else h_bufs[i][:, hf * HALF : (hf + 1) * HALF]
+
         def write_entries(i):
             c = [n for n, (c0, c1) in enumerate(W1_CHUNKS) if c0 <= i * P < c1][0]
             codes, scales, width = w1_mx[c]
             first = i * P - W1_CHUNKS[c][0]
-            h = h_bufs[i % H_BUFS]
             for hf in range(2):
                 for a in range(PASSES):
                     cols = slice(a * width + first, a * width + first + P)
@@ -168,21 +166,21 @@ def tile_list_hive_diary_kernel(
                         start=(a == 0),
                         stop=(a == PASSES - 1),
                     )
-                nc.scalar.copy(out=h[:, hf * HALF : (hf + 1) * HALF], in_=h_banks[hf][:])
-
-        def put(i):
-            h = h_bufs[i % H_BUFS]
-            pieces = [(0, HALF), (HALF, S)] if i == 0 else [(0, S)]
-            for j0, j1 in pieces:
+                nc.scalar.copy(out=h_half(i, hf), in_=h_banks[hf][:])
+            if i == 0:
+                pieces = [(h_half(0, hf), hf * HALF, (hf + 1) * HALF) for hf in range(2)]
+            else:
+                pieces = [(h_bufs[i], 0, S)]
+            for h, j0, j1 in pieces:
                 nc.vector.tensor_tensor(
-                    pages[i][:].indirect(put_list[:, j0 // 16 : j1 // 16]), h[:, j0:j1], wgs_sb[:, j0:j1], MULT
+                    pages[i][:].indirect(put_list[:, j0 // 16 : j1 // 16]), h, wgs_sb[:, j0:j1], MULT
                 )
 
         z_ring = [held(f"zt{n}", [P, PACK * BANK], BF16) for n in range(2)]
         z_codes = [[held(f"zc{c}_{b}", [P, m1 - m0], U32) for b in range(PASSES)] for c, (m0, m1) in enumerate(CHUNKS)]
         z_scales = [[held(f"zs{c}_{b}", [P, m1 - m0], U8) for b in range(PASSES)] for c, (m0, m1) in enumerate(CHUNKS)]
-        scaled = h_bufs[0:NS]
-        late_x = [h_bufs[ROW_TILES - 1], wgs_sb, h_bufs[ROW_TILES - 2]]
+        scaled = [rooms[0][:, low], rooms[2][:, low], rooms[2][:, high]]
+        late_x = [h_bufs[ROW_TILES - 1], wgs_sb]
 
         def z_t(c, b):
             width = CHUNKS[c][1] - CHUNKS[c][0]
@@ -273,7 +271,10 @@ def tile_list_hive_diary_kernel(
             m0, m1 = CHUNKS[c]
             width = m1 - m0
             cols = slice(0, len(tiles) * width)
-            size, root, part = [h_bufs[n][:, (u % 2) * BANK : (u % 2 + 1) * BANK] for n in (3, 4, 5)]
+            size, root, part = [
+                room[:, (u % 2) * BANK : (u % 2 + 1) * BANK]
+                for room in (rooms[1][:, low], rooms[1][:, high], rooms[3][:, low])
+            ]
             result = stage.tile([P, BANK], F32, name="result", tag="result", bufs=3)
 
             def sums():
@@ -298,12 +299,14 @@ def tile_list_hive_diary_kernel(
 
         w3_mx = []
         for i in range(ROW_TILES):
-            if i + 1 < len(W1_CHUNKS):
-                w1_mx.append(quantize_weight(f"w1_{i + 1}", w1_raw[i + 1]))
-            elif len(w3_mx) < 2:
-                w3_mx.append(quantize_weight(f"w3_{i}", w3_raw[len(w3_mx)]))
+            if i % 2 == 1 and len(w1_mx) < len(W1_CHUNKS):
+                c = len(w1_mx)
+                w1_mx.append(quantize_weight(f"w1_{c}", w1_raw[c], casts[c % 2]))
             write_entries(i)
-            put(i)
+            if i in (4, 5):
+                c = i - 4
+                w3_raw = load_weight(w3, c * N // 2, (c + 1) * N // 2, rooms[1 + 2 * c])
+                w3_mx.append(quantize_weight(f"w3_{c}", w3_raw, casts[c]))
         nc.tensor.transpose(h_banks[1][:, 0:P], lam_rows[:], ident[:])
         nc.scalar.copy(out=lam_cols[:], in_=h_banks[1][:, 0:ROW_TILES])
         nc.scalar.activation(out=rest_cols[:], in_=h_banks[1][:, 0:ROW_TILES], func=ACT.Copy, scale=-1.0, bias=1.0)

@@ -3,8 +3,8 @@ from contextlib import ExitStack
 import concourse.mybir as mybir
 from concourse.masks import make_identity
 
-K, H, N, T, S, T2, PM = 1024, 1024, 512, 2048, 1024, 2048, 1024
-FLOPS = 2 * K * H * S + 2 * 2 * H * N * PM
+K, H, N, T, S, T2, TREATMENTS = 1024, 1024, 512, 2048, 1024, 2048, 1024
+FLOPS = 2 * K * H * S + 2 * 2 * H * N * TREATMENTS
 
 F32 = mybir.dt.float32
 BF16 = mybir.dt.bfloat16
@@ -22,15 +22,18 @@ PACK = 4
 K_PASS = P * PACK
 PASSES = 2
 BANK = 512
+QUADRANTS = 4
+LIST_ROWS = 16
 ROW_TILES = H // P
 HALF = S // 2
-W1_CHUNKS = [(0, 256), (256, 512), (512, 768), (768, 1024)]
+W_COLS = 256
 CHUNKS = [(0, 512), (512, 768), (768, 1024)]
-X_SLOTS = 2
-LAG = 2
-NS = 3
-QL = 1
-ST = 6
+SUM_BANKS = 3
+COLLECT_LAG = 2
+QUANTISE_LAG = 3
+FIRST_SCORE_TURN = 14
+SCORE_SLOTS = 4
+RESULT_BUFS = 6
 
 
 def tile_list_hive_diary_kernel(
@@ -45,12 +48,16 @@ def tile_list_hive_diary_kernel(
         def held(name, shape, dtype):
             return keep.tile(shape, dtype, name=name, align_bytes=64)
 
-        lists = [keep.tile([P, S // 16], U16, name=f"list{n}") for n in range(4)]
-        tab_list, put_list, before_list, after_list = lists
+        def entries(offsets, first, end):
+            return offsets[:, first // LIST_ROWS : end // LIST_ROWS]
+
+        tab_list, put_list, before_list, after_list = [
+            keep.tile([P, S // LIST_ROWS], U16, name=f"list{n}") for n in range(4)
+        ]
         words = [held(f"words{a}", [P, T], U32) for a in range(PASSES)]
         planes = held("planes", [P, T], U8)
-        picked_words = [[held(f"pw{a}_{hf}", [P, HALF], U32) for hf in range(2)] for a in range(PASSES)]
-        picked_planes = [held(f"pp{hf}", [P, HALF], U8) for hf in range(2)]
+        picked_words = [[held(f"picked_words{a}_{hf}", [P, HALF], U32) for hf in range(2)] for a in range(PASSES)]
+        picked_planes = [held(f"picked_planes{hf}", [P, HALF], U8) for hf in range(2)]
         pages = [held(f"page{i}", [P, T2], F32) for i in range(ROW_TILES)]
         wgs_sb = held("wgs_sb", [P, S], F32)
         lam_rows = held("lam_rows", [P, P], F32)
@@ -60,58 +67,69 @@ def tile_list_hive_diary_kernel(
         ident = held("ident", [P, P], F32)
         w2_codes = held("w2_codes", [P, PASSES, 2 * N], U8)
         w2_planes = held("w2_planes", [P, PASSES, N], U8)
-        rooms = [held(f"room{c}", [P, PASSES * PACK * (c1 - c0)], F32) for c, (c0, c1) in enumerate(W1_CHUNKS)]
+
+        rooms = [held(f"room{c}", [P, PASSES * PACK * W_COLS], F32) for c in range(H // W_COLS)]
         casts = [held(f"cast{n}", [P, S], F32) for n in range(2)]
         low, high = slice(0, S), slice(S, 2 * S)
-        h_bufs = [None, rooms[1][:, high], rooms[0][:, low], rooms[2][:, high], rooms[1][:, low], rooms[3][:, high],
-                  rooms[2][:, low], rooms[0][:, high]]
+        h_bufs = {
+            i: rooms[(i + 1) // 2 % len(rooms)][:, high] if i % 2 == 1 else rooms[i // 2 - 1][:, low]
+            for i in range(1, ROW_TILES)
+        }
+
         banks = [psum.tile([P, BANK], F32, name=f"bank{b}") for b in range(8)]
-        h_banks, sum_banks, word_banks = banks[0:2], banks[2:2+NS], banks[2+NS:6]
-        den_banks, num_banks = [banks[6], banks[0]], [banks[7], banks[1]]
+        h_banks, sum_banks, word_bank = banks[0:2], banks[2 : 2 + SUM_BANKS], banks[5]
 
-        def load_weight(w, c0, c1, room):
-            size = PACK * (c1 - c0)
-            raws = [room[:, a * size : (a + 1) * size].rearrange("p (j c) -> p j c", j=PACK) for a in range(PASSES)]
-            for a in range(PASSES):
-                rows = w[a * K_PASS : (a + 1) * K_PASS, c0:c1].rearrange("(p j) c -> p j c", j=PACK)
-                nc.sync.dma_start(out=raws[a], in_=rows)
-            return raws
-
-        def quantize_weight(name, raws, cast):
-            width = raws[0].shape[2]
-            values = PASSES * PACK * width
-            grouped = cast[:].bitcast(BF16)[:, 2 * S - values : 2 * S]
-            for a in range(PASSES):
-                nc.scalar.copy(
-                    out=grouped[:, a * PACK * width : (a + 1) * PACK * width].rearrange("p (c i j) -> p c j i", i=4, j=PACK),
-                    in_=raws[a].rearrange("p j (c i) -> p c j i", i=4),
-                )
-            codes = held(f"{name}_codes", [P, PASSES * width], U32)
-            scales = held(f"{name}_scales", [P, PASSES * width], U8)
-            nc.vector.quantize_mx(out=codes[:].bitcast(FP8X4), scales=scales[:], in_=grouped)
-            return codes, scales, width
+        def load_words(a):
+            source = tab_words[a].rearrange("p t i -> p (t i)").bitcast(I32)
+            nc.sync.dma_start(out=words[a][:].bitcast(I32), in_=source)
 
         def load_page(i):
             nc.sync.dma_start(out=pages[i][:], in_=page0[i * P : (i + 1) * P, :])
+
+        def load_weight(w, c, room):
+            size = PACK * W_COLS
+            raws = [room[:, a * size : (a + 1) * size].rearrange("p (j c) -> p j c", j=PACK) for a in range(PASSES)]
+            for a in range(PASSES):
+                rows = w[a * K_PASS : (a + 1) * K_PASS, c * W_COLS : (c + 1) * W_COLS]
+                nc.sync.dma_start(out=raws[a], in_=rows.rearrange("(p j) c -> p j c", j=PACK))
+            return raws
+
+        def quantise_weight(name, raws, cast):
+            size = PACK * W_COLS
+            grouped = cast[:].bitcast(BF16)[:, 0 : PASSES * size]
+            for a in range(PASSES):
+                nc.scalar.copy(
+                    out=grouped[:, a * size : (a + 1) * size].rearrange("p (c i j) -> p c j i", i=4, j=PACK),
+                    in_=raws[a].rearrange("p j (c i) -> p c j i", i=4),
+                )
+            codes = held(f"{name}_codes", [P, PASSES * W_COLS], U32)
+            scales = held(f"{name}_scales", [P, PASSES * W_COLS], U8)
+            nc.vector.quantize_mx(out=codes[:].bitcast(FP8X4), scales=scales[:], in_=grouped)
+            return codes, scales
+
+        def stationary(weight_mx, tile, a):
+            codes, scales = weight_mx[tile * P // W_COLS]
+            first = a * W_COLS + tile * P % W_COLS
+            return codes[:, first : first + P].bitcast(FP8X4), scales[:, first : first + P]
 
         nc.gpsimd.memset(planes[:].bitcast(I32), 0)
         nc.gpsimd.memset(one[:], 1.0)
         warm = held("warm", [P, 1], F32)
         nc.scalar.activation(out=warm[:], in_=one[:], func=ACT.Abs_reciprocal_sqrt, bias=one[:])
         nc.sync.dma_start(tab_list[:], offs)
-        for q in range(4):
+        for q in range(QUADRANTS):
             nc.sync.dma_start(
                 out=planes[32 * q : 32 * q + 4 * PASSES, :].bitcast(I32),
                 in_=tab_scales[:, 4 * q : 4 * q + 4, :].bitcast(I32),
             )
-        nc.sync.dma_start(out=words[0][:].bitcast(I32), in_=tab_words[0].rearrange("p t i -> p (t i)").bitcast(I32))
-        w1_raw = [load_weight(w1, *W1_CHUNKS[0], rooms[0])]
-        nc.sync.dma_start(out=words[1][:].bitcast(I32), in_=tab_words[1].rearrange("p t i -> p (t i)").bitcast(I32))
+        load_words(0)
+        w1_raw = [load_weight(w1, 0, rooms[0])]
+        load_words(1)
         nc.sync.dma_start(out=wgs_sb[:], in_=wgs)
         nc.sync.dma_start(put_list[:], offs2)
         load_page(0)
-        for c in range(1, len(W1_CHUNKS)):
-            w1_raw.append(load_weight(w1, *W1_CHUNKS[c], rooms[c]))
+        for c in range(1, len(rooms)):
+            w1_raw.append(load_weight(w1, c, rooms[c]))
             load_page(c)
         load_page(4)
         load_page(5)
@@ -123,7 +141,7 @@ def tile_list_hive_diary_kernel(
         load_page(6)
         load_page(7)
         nc.gpsimd.memset(w2_planes[:].bitcast(I32), 0)
-        for q in range(4):
+        for q in range(QUADRANTS):
             nc.sync.dma_start(
                 out=w2_planes[32 * q : 32 * q + 4, :, :].bitcast(I32),
                 in_=w2_scales[:, 4 * q : 4 * q + 4, :].rearrange("a r c -> r a c").bitcast(I32),
@@ -131,215 +149,196 @@ def tile_list_hive_diary_kernel(
         make_identity(nc, ident[:])
 
         def pick_words(a, hf):
-            cols = tab_list[:, hf * HALF // 16 : (hf + 1) * HALF // 16]
-            nc.vector.tensor_copy(picked_words[a][hf][:], words[a][:].indirect(cols))
+            picks = entries(tab_list, hf * HALF, (hf + 1) * HALF)
+            nc.vector.tensor_copy(picked_words[a][hf][:], words[a][:].indirect(picks))
 
         def pick_planes(hf):
-            cols = tab_list[:, hf * HALF // 16 : (hf + 1) * HALF // 16]
-            nc.vector.tensor_copy(picked_planes[hf][:], planes[:].indirect(cols))
+            picks = entries(tab_list, hf * HALF, (hf + 1) * HALF)
+            nc.vector.tensor_copy(picked_planes[hf][:], planes[:].indirect(picks))
 
         pick_planes(0)
         pick_words(0, 0)
         pick_words(1, 0)
-        w1_mx = [quantize_weight("w1_0", w1_raw[0], casts[0])]
+        w1_mx = [quantise_weight("w1_0", w1_raw[0], casts[0])]
         pick_planes(1)
         pick_words(0, 1)
         pick_words(1, 1)
 
-
-        def h_half(i, hf):
-            return casts[1 - hf][:, HALF // 2 : HALF // 2 + HALF] if i == 0 else h_bufs[i][:, hf * HALF : (hf + 1) * HALF]
-
         def write_entries(i):
-            c = [n for n, (c0, c1) in enumerate(W1_CHUNKS) if c0 <= i * P < c1][0]
-            codes, scales, width = w1_mx[c]
-            first = i * P - W1_CHUNKS[c][0]
+            if i == 0:
+                halves = [casts[1 - hf][:, HALF // 2 : HALF // 2 + HALF] for hf in range(2)]
+                pieces = [(halves[hf], hf * HALF, (hf + 1) * HALF) for hf in range(2)]
+            else:
+                halves = [h_bufs[i][:, hf * HALF : (hf + 1) * HALF] for hf in range(2)]
+                pieces = [(h_bufs[i], 0, S)]
             for hf in range(2):
                 for a in range(PASSES):
-                    cols = slice(a * width + first, a * width + first + P)
+                    codes, scales = stationary(w1_mx, i, a)
                     nc.tensor.matmul_mx(
                         out=h_banks[hf][:],
-                        lhsT=codes[:, cols].bitcast(FP8X4),
-                        lhsT_scale=scales[:, cols],
+                        lhsT=codes,
+                        lhsT_scale=scales,
                         rhs=picked_words[a][hf][:].bitcast(FP8X4),
                         rhs_scale=picked_planes[hf][4 * a : P, :],
                         start=(a == 0),
                         stop=(a == PASSES - 1),
                     )
-                nc.scalar.copy(out=h_half(i, hf), in_=h_banks[hf][:])
-            if i == 0:
-                pieces = [(h_half(0, hf), hf * HALF, (hf + 1) * HALF) for hf in range(2)]
-            else:
-                pieces = [(h_bufs[i], 0, S)]
-            for h, j0, j1 in pieces:
-                nc.vector.tensor_tensor(
-                    pages[i][:].indirect(put_list[:, j0 // 16 : j1 // 16]), h, wgs_sb[:, j0:j1], MULT
-                )
+                nc.scalar.copy(out=halves[hf], in_=h_banks[hf][:])
+            for h, first, end in pieces:
+                days = pages[i][:].indirect(entries(put_list, first, end))
+                nc.vector.tensor_tensor(h, h, wgs_sb[:, first:end], MULT)
+                nc.vector.tensor_copy(days, h)
 
-        z_ring = [held(f"zt{n}", [P, PACK * BANK], BF16) for n in range(2)]
-        z_codes = [[held(f"zc{c}_{b}", [P, m1 - m0], U32) for b in range(PASSES)] for c, (m0, m1) in enumerate(CHUNKS)]
-        z_scales = [[held(f"zs{c}_{b}", [P, m1 - m0], U8) for b in range(PASSES)] for c, (m0, m1) in enumerate(CHUNKS)]
-        scaled = [rooms[0][:, low], rooms[2][:, low], rooms[2][:, high]]
-        late_x = [h_bufs[ROW_TILES - 1], wgs_sb]
+        w3_mx = []
+        for i in range(ROW_TILES):
+            if i % 2 == 1 and len(w1_mx) < len(rooms):
+                c = len(w1_mx)
+                w1_mx.append(quantise_weight(f"w1_{c}", w1_raw[c], casts[c % 2]))
+            write_entries(i)
+            if i in (4, 5):
+                c = i - 4
+                w3_mx.append(quantise_weight(f"w3_{c}", load_weight(w3, c, rooms[1 + 2 * c]), casts[c]))
 
-        def z_t(c, b):
-            width = CHUNKS[c][1] - CHUNKS[c][0]
-            return z_ring[b][:, 0 : PACK * width]
+        nc.tensor.transpose(h_banks[1][:, 0:P], lam_rows[:], ident[:])
+        nc.scalar.copy(out=lam_cols[:], in_=h_banks[1][:, 0:ROW_TILES])
+        nc.scalar.activation(out=rest_cols[:], in_=h_banks[1][:, 0:ROW_TILES], func=ACT.Copy, scale=-1.0, bias=1.0)
 
-        def fetch(c, i):
-            m0, m1 = CHUNKS[c]
-            width = m1 - m0
-            turn = c * ROW_TILES + i
-            x = late_x[turn % X_SLOTS]
-            y = scaled[turn % NS]
-            bank = sum_banks[turn % NS]
-            for n, (visits, weight) in enumerate(((before_list, rest_cols), (after_list, lam_cols))):
+        widths = [end - first for first, end in CHUNKS]
+        z_rows = [held(f"z_rows{b}", [P, PACK * BANK], BF16) for b in range(PASSES)]
+        z_codes = [[held(f"z_codes{c}_{b}", [P, w], U32) for b in range(PASSES)] for c, w in enumerate(widths)]
+        z_scales = [[held(f"z_scales{c}_{b}", [P, w], U8) for b in range(PASSES)] for c, w in enumerate(widths)]
+        weighted = [rooms[0][:, low], rooms[2][:, low], rooms[2][:, high]]
+        visits = [h_bufs[ROW_TILES - 1], wgs_sb]
+
+        def fetch(turn):
+            c, i = divmod(turn, ROW_TILES)
+            width = widths[c]
+            raw, scaled, bank = visits[turn % 2], weighted[turn % SUM_BANKS], sum_banks[turn % SUM_BANKS]
+            for n, (days, weight) in enumerate(((before_list, rest_cols), (after_list, lam_cols))):
                 cols = slice(n * width, (n + 1) * width)
-                nc.vector.tensor_copy(x[:, cols], pages[i][:].indirect(visits[:, m0 // 16 : m1 // 16]))
-                nc.scalar.activation(out=y[:, cols], in_=x[:, cols], func=ACT.Copy, scale=weight[:, i : i + 1])
+                nc.vector.tensor_copy(raw[:, cols], pages[i][:].indirect(entries(days, *CHUNKS[c])))
+                nc.scalar.activation(out=scaled[:, cols], in_=raw[:, cols], func=ACT.Copy, scale=weight[:, i : i + 1])
             for j in range(width // P):
                 for n in (1, 0):
                     nc.tensor.matmul(
                         bank[:, j * P : (j + 1) * P],
-                        y[:, n * width + j * P : n * width + (j + 1) * P],
+                        scaled[:, n * width + j * P : n * width + (j + 1) * P],
                         ident[:],
                         is_transpose=True,
                         start=(n == 1),
                         stop=(n == 0),
                     )
 
-        def collect(c, i):
-            width = CHUNKS[c][1] - CHUNKS[c][0]
-            bank = sum_banks[(c * ROW_TILES + i) % NS]
-            quarter = i % PACK
+        def collect(turn):
+            c, i = divmod(turn, ROW_TILES)
+            b, quarter = divmod(i, PACK)
+            rows = z_rows[b][:, 0 : PACK * widths[c]].rearrange("m (u j p e) -> m u j p e", u=2, p=P, e=2)
             nc.scalar.copy(
-                out=z_t(c, i // PACK).rearrange("m (u j p e) -> m u j p e", u=2, p=P, e=2)[
-                    :, :, :, 32 * quarter : 32 * (quarter + 1), :
-                ],
-                in_=bank[:, 0:width].rearrange("m (j p u e) -> m u j p e", p=32, u=2, e=2),
+                out=rows[:, :, :, 32 * quarter : 32 * (quarter + 1), :],
+                in_=sum_banks[turn % SUM_BANKS][:, 0 : widths[c]].rearrange("m (j p u e) -> m u j p e", p=32, u=2, e=2),
             )
 
-        def quantize_z(c, b):
-            m0, m1 = CHUNKS[c]
-            blocks = (m1 - m0) // P
-            pairs = z_t(c, b).bitcast(F32)
-            grouped = stage.tile([P, (m1 - m0) * PACK], BF16, name="z_grouped", tag="z_grouped", align_bytes=64)
+        def quantise_z(c, b):
+            blocks = widths[c] // P
+            pairs = z_rows[b][:, 0 : PACK * widths[c]].bitcast(F32)
+            grouped = stage.tile([P, widths[c] * PACK], BF16, name="z_grouped", tag="z_grouped", align_bytes=64)
             for j0 in range(0, blocks, 2):
-                bank = word_banks[(b + j0 // 2) % len(word_banks)]
-                for jj in range(2):
+                for j in range(2):
                     for u in range(2):
-                        src = (u * blocks + j0 + jj) * P
-                        dst = (jj * 2 + u) * P
-                        nc.tensor.transpose(bank[:, dst : dst + P], pairs[:, src : src + P], ident[:])
+                        source, target = (u * blocks + j0 + j) * P, (2 * j + u) * P
+                        nc.tensor.transpose(word_bank[:, target : target + P], pairs[:, source : source + P], ident[:])
+                grouped_words = grouped[:].bitcast(F32)[:, j0 * 2 * P : (j0 + 2) * 2 * P]
                 nc.scalar.copy(
-                    out=grouped[:].bitcast(F32)[:, j0 * 2 * P : (j0 + 2) * 2 * P].rearrange("p (j m u) -> p j m u", j=2, u=2),
-                    in_=bank[:].rearrange("p (j u m) -> p j m u", j=2, u=2),
+                    out=grouped_words.rearrange("p (j m u) -> p j m u", j=2, u=2),
+                    in_=word_bank[:].rearrange("p (j u m) -> p j m u", j=2, u=2),
                 )
             nc.vector.quantize_mx(out=z_codes[c][b][:].bitcast(FP8X4), scales=z_scales[c][b][:], in_=grouped[:])
 
-        def den_sums(c, nt, bank, first):
-            width = CHUNKS[c][1] - CHUNKS[c][0]
-            codes, scales, w3_width = w3_mx[nt // 2]
+        def den_sums(c, tile, target):
             for b in range(PASSES):
-                cols = slice(b * w3_width + (nt % 2) * P, b * w3_width + (nt % 2 + 1) * P)
+                codes, scales = stationary(w3_mx, tile, b)
                 nc.tensor.matmul_mx(
-                    out=bank[:, first : first + width],
-                    lhsT=codes[:, cols].bitcast(FP8X4),
-                    lhsT_scale=scales[:, cols],
+                    out=target,
+                    lhsT=codes,
+                    lhsT_scale=scales,
                     rhs=z_codes[c][b][:].bitcast(FP8X4),
                     rhs_scale=z_scales[c][b][:],
                     start=(b == 0),
                     stop=(b == PASSES - 1),
                 )
 
-        def num_sums(c, nt, bank, first):
-            width = CHUNKS[c][1] - CHUNKS[c][0]
-            step = BANK if width == BANK else P
-            for g0 in range(0, width, step):
+        def num_sums(c, tile, target):
+            step = BANK if widths[c] == BANK else P
+            for first in range(0, widths[c], step):
+                cols = slice(first, first + step)
                 for b in range(PASSES):
                     nc.tensor.matmul_mx(
-                        out=bank[:, first + g0 : first + g0 + step],
-                        lhsT=w2_codes[:, b, 2 * nt * P : 2 * (nt + 1) * P].bitcast(FP4X4),
-                        lhsT_scale=w2_planes[:, b, nt * P : (nt + 1) * P],
-                        rhs=z_codes[c][b][:, g0 : g0 + step].bitcast(FP8X4),
-                        rhs_scale=z_scales[c][b][:, g0 : g0 + step],
+                        out=target[:, cols],
+                        lhsT=w2_codes[:, b, 2 * tile * P : 2 * (tile + 1) * P].bitcast(FP4X4),
+                        lhsT_scale=w2_planes[:, b, tile * P : (tile + 1) * P],
+                        rhs=z_codes[c][b][:, cols].bitcast(FP8X4),
+                        rhs_scale=z_scales[c][b][:, cols],
                         start=(b == 0),
                         stop=(b == PASSES - 1),
                     )
 
-        def score_steps(u, c, tiles, den, num):
-            m0, m1 = CHUNKS[c]
-            width = m1 - m0
+        def score_steps(unit, c, tiles, den, num):
+            width = widths[c]
             cols = slice(0, len(tiles) * width)
-            size, root, part = [
-                room[:, (u % 2) * BANK : (u % 2 + 1) * BANK]
-                for room in (rooms[1][:, low], rooms[1][:, high], rooms[3][:, low])
-            ]
-            result = stage.tile([P, BANK], F32, name="result", tag="result", bufs=3)
+            slot = (unit % SCORE_SLOTS) * BANK
+            size = casts[unit % 2][:, cols]
+            root = rooms[1][:, slot : slot + BANK][:, cols]
+            part = rooms[3][:, slot : slot + BANK][:, cols]
+            result = stage.tile([P, BANK], F32, name="result", tag="result", bufs=RESULT_BUFS)
 
             def sums():
-                for n, nt in enumerate(tiles):
-                    den_sums(c, nt, den, n * width)
-                for n, nt in enumerate(tiles):
-                    num_sums(c, nt, num, n * width)
-                nc.scalar.activation(out=size[:, cols], in_=den[:, cols], func=ACT.Abs)
+                for n, tile in enumerate(tiles):
+                    den_sums(c, tile, den[:, n * width : (n + 1) * width])
+                for n, tile in enumerate(tiles):
+                    num_sums(c, tile, num[:, n * width : (n + 1) * width])
+                nc.scalar.activation(out=size, in_=den[:, cols], func=ACT.Abs)
 
             def inverse_root():
-                nc.scalar.activation(out=root[:, cols], in_=size[:, cols], func=ACT.Abs_reciprocal_sqrt, bias=one[:])
+                nc.scalar.activation(out=root, in_=size, func=ACT.Abs_reciprocal_sqrt, bias=one[:])
 
-            def finish():
-                nc.vector.tensor_tensor(part[:, cols], num[:, cols], root[:, cols], MULT)
-                nc.vector.tensor_tensor(result[:, cols], part[:, cols], root[:, cols], MULT)
+            def first_product():
+                nc.vector.tensor_tensor(part, num[:, cols], root, MULT)
+
+            def second_product():
+                nc.vector.tensor_tensor(result[:, cols], part, root, MULT)
+                rows = out[tiles[0] * P : (tiles[-1] + 1) * P, CHUNKS[c][0] : CHUNKS[c][1]]
                 nc.sync.dma_start(
-                    out=out[tiles[0] * P : (tiles[-1] + 1) * P, m0:m1].rearrange("(t p) m -> p t m", p=P),
+                    out=rows.rearrange("(t p) m -> p t m", p=P),
                     in_=result[:, cols].rearrange("p (t m) -> p t m", t=len(tiles)),
                 )
 
-            return [sums, inverse_root, finish]
+            return [sums, inverse_root, first_product, second_product]
 
-        w3_mx = []
-        for i in range(ROW_TILES):
-            if i % 2 == 1 and len(w1_mx) < len(W1_CHUNKS):
-                c = len(w1_mx)
-                w1_mx.append(quantize_weight(f"w1_{c}", w1_raw[c], casts[c % 2]))
-            write_entries(i)
-            if i in (4, 5):
-                c = i - 4
-                w3_raw = load_weight(w3, c * N // 2, (c + 1) * N // 2, rooms[1 + 2 * c])
-                w3_mx.append(quantize_weight(f"w3_{c}", w3_raw, casts[c]))
-        nc.tensor.transpose(h_banks[1][:, 0:P], lam_rows[:], ident[:])
-        nc.scalar.copy(out=lam_cols[:], in_=h_banks[1][:, 0:ROW_TILES])
-        nc.scalar.activation(out=rest_cols[:], in_=h_banks[1][:, 0:ROW_TILES], func=ACT.Copy, scale=-1.0, bias=1.0)
-        last = len(CHUNKS) - 1
+        out_tiles = N // P
+        bank_pairs = [(banks[6], banks[7]), (banks[0], banks[1])]
         units = []
-        for c in range(last):
-            group = BANK // (CHUNKS[c][1] - CHUNKS[c][0])
-            for nt in range(0, N // P, group):
-                units.append((c, list(range(nt, nt + group)), den_banks[len(units) % 2], num_banks[len(units) % 2]))
-        tail_den = [banks[2], banks[3], banks[6], banks[0]]
-        tail_num = [banks[4], banks[5], banks[7], banks[1]]
-        for nt in range(N // P):
-            units.append((last, [nt], tail_den[nt], tail_num[nt]))
-        waiting = []
-        for n, unit in enumerate(units):
-            steps = score_steps(n, *unit)
-            waiting.append(steps)
-        queue = []
-        for n in range(len(units) + 2):
-            for k in (2, 1, 0):
-                if 0 <= n - k < len(units):
-                    queue.append((units[n - k][0], waiting[n - k][k]))
+        for c in range(len(CHUNKS) - 1):
+            group = BANK // widths[c]
+            for tile in range(0, out_tiles, group):
+                units.append((c, list(range(tile, tile + group)), *bank_pairs[len(units) % 2]))
+        for tile, pair in enumerate([(banks[2], banks[4]), (banks[3], banks[5])] + bank_pairs):
+            units.append((len(CHUNKS) - 1, [tile], *pair))
+        steps = [score_steps(unit, *what) for unit, what in enumerate(units)]
+        queue = [
+            steps[n - k][k] for n in range(len(units) + 3) for k in (2, 3, 1, 0) if 0 <= n - k < len(units)
+        ]
+
         turns = len(CHUNKS) * ROW_TILES
-        for turn in range(turns + LAG + QL):
+        for turn in range(turns + QUANTISE_LAG):
             if turn < turns:
-                fetch(*divmod(turn, ROW_TILES))
-            if 0 <= turn - LAG < turns:
-                collect(*divmod(turn - LAG, ROW_TILES))
-            c, i = divmod(turn - LAG - QL, ROW_TILES)
+                fetch(turn)
+            if 0 <= turn - COLLECT_LAG < turns:
+                collect(turn - COLLECT_LAG)
+            c, i = divmod(turn - QUANTISE_LAG, ROW_TILES)
             if c >= 0 and i % PACK == PACK - 1:
-                quantize_z(c, i // PACK)
-            elif turn >= ROW_TILES + ST and turn < turns and queue[0][0] < len(CHUNKS) - 1:
-                queue[0][1]()
+                quantise_z(c, i // PACK)
+            elif FIRST_SCORE_TURN <= turn < turns:
+                queue[0]()
                 queue = queue[1:]
-        for c, step in queue:
+        for step in queue:
             step()

@@ -186,8 +186,7 @@ def tile_list_hive_diary_kernel(
                 nc.scalar.copy(out=halves[hf], in_=h_banks[hf][:])
             for h, first, end in pieces:
                 days = pages[i][:].indirect(entries(put_list, first, end))
-                nc.vector.tensor_tensor(h, h, wgs_sb[:, first:end], MULT)
-                nc.vector.tensor_copy(days, h)
+                nc.vector.tensor_tensor(days, h, wgs_sb[:, first:end], MULT)
 
         w3_mx = []
         for i in range(ROW_TILES):

@@ -28,11 +28,14 @@ ROW_TILES = H // P
 HALF = S // 2
 W_COLS = 256
 CHUNKS = [(0, 512), (512, 768), (768, 1024)]
-SUM_BANKS = 3
-COLLECT_LAG = 2
-QUANTISE_LAG = 3
-FIRST_SCORE_TURN = 14
+SUM_BANKS = 2
+COLLECT_LAG = 1
+QUANTISE_LAG = 1
+FIRST_SCORE_TURN = 12
 SCORE_SLOTS = 4
+STEPS_A_TURN = 1
+RING = 3
+SQUARED_UNITS = 4
 RESULT_BUFS = 6
 
 
@@ -62,7 +65,7 @@ def tile_list_hive_diary_kernel(
         wgs_sb = held("wgs_sb", [P, S], F32)
         lam_rows = held("lam_rows", [P, P], F32)
         lam_cols = held("lam_cols", [P, ROW_TILES], F32)
-        rest_cols = held("rest_cols", [P, ROW_TILES], F32)
+        weights = [[held(f"weight{n}_{i}", [P, BANK], F32) for i in range(ROW_TILES)] for n in range(2)]
         one = held("one", [P, 1], F32)
         ident = held("ident", [P, P], F32)
         w2_codes = held("w2_codes", [P, PASSES, 2 * N], U8)
@@ -77,7 +80,7 @@ def tile_list_hive_diary_kernel(
         }
 
         banks = [psum.tile([P, BANK], F32, name=f"bank{b}") for b in range(8)]
-        h_banks, sum_banks, word_bank = banks[0:2], banks[2 : 2 + SUM_BANKS], banks[5]
+        h_banks, sum_banks, word_banks = banks[0:2], banks[2 : 2 + SUM_BANKS], banks[4:5]
 
         def load_words(a):
             source = tab_words[a].rearrange("p t i -> p (t i)").bitcast(I32)
@@ -200,23 +203,26 @@ def tile_list_hive_diary_kernel(
 
         nc.tensor.transpose(h_banks[1][:, 0:P], lam_rows[:], ident[:])
         nc.scalar.copy(out=lam_cols[:], in_=h_banks[1][:, 0:ROW_TILES])
-        nc.scalar.activation(out=rest_cols[:], in_=h_banks[1][:, 0:ROW_TILES], func=ACT.Copy, scale=-1.0, bias=1.0)
+        for i in range(ROW_TILES):
+            spread = lam_cols[:, i : i + 1].to_broadcast([P, BANK])
+            nc.scalar.activation(out=weights[0][i][:], in_=spread, func=ACT.Copy, scale=-1.0, bias=1.0)
+            nc.scalar.copy(out=weights[1][i][:], in_=spread)
 
         widths = [end - first for first, end in CHUNKS]
         z_rows = [held(f"z_rows{b}", [P, PACK * BANK], BF16) for b in range(PASSES)]
         z_codes = [[held(f"z_codes{c}_{b}", [P, w], U32) for b in range(PASSES)] for c, w in enumerate(widths)]
         z_scales = [[held(f"z_scales{c}_{b}", [P, w], U8) for b in range(PASSES)] for c, w in enumerate(widths)]
-        weighted = [rooms[0][:, low], rooms[2][:, low], rooms[2][:, high]]
         visits = [h_bufs[ROW_TILES - 1], wgs_sb]
 
         def fetch(turn):
             c, i = divmod(turn, ROW_TILES)
             width = widths[c]
-            raw, scaled, bank = visits[turn % 2], weighted[turn % SUM_BANKS], sum_banks[turn % SUM_BANKS]
-            for n, (days, weight) in enumerate(((before_list, rest_cols), (after_list, lam_cols))):
-                cols = slice(n * width, (n + 1) * width)
-                nc.vector.tensor_copy(raw[:, cols], pages[i][:].indirect(entries(days, *CHUNKS[c])))
-                nc.scalar.activation(out=scaled[:, cols], in_=raw[:, cols], func=ACT.Copy, scale=weight[:, i : i + 1])
+            piece, which = divmod(turn % min(RING, S // width), 2)
+            scaled = visits[which][:, piece * 2 * width : (piece + 1) * 2 * width]
+            bank = sum_banks[turn % SUM_BANKS]
+            for n, days in enumerate((before_list, after_list)):
+                visit = pages[i][:].indirect(entries(days, *CHUNKS[c]))
+                nc.vector.tensor_tensor(scaled[:, n * width : (n + 1) * width], visit, weights[n][i][:, 0:width], MULT)
             for j in range(width // P):
                 for n in (1, 0):
                     nc.tensor.matmul(
@@ -242,6 +248,7 @@ def tile_list_hive_diary_kernel(
             pairs = z_rows[b][:, 0 : PACK * widths[c]].bitcast(F32)
             grouped = stage.tile([P, widths[c] * PACK], BF16, name="z_grouped", tag="z_grouped", align_bytes=64)
             for j0 in range(0, blocks, 2):
+                word_bank = word_banks[(j0 // 2 + b) % len(word_banks)]
                 for j in range(2):
                     for u in range(2):
                         source, target = (u * blocks + j0 + j) * P, (2 * j + u) * P
@@ -267,7 +274,7 @@ def tile_list_hive_diary_kernel(
                 )
 
         def num_sums(c, tile, target):
-            step = BANK if widths[c] == BANK else P
+            step = widths[c]
             for first in range(0, widths[c], step):
                 cols = slice(first, first + step)
                 for b in range(PASSES):
@@ -301,10 +308,14 @@ def tile_list_hive_diary_kernel(
                 nc.scalar.activation(out=root, in_=size, func=ACT.Abs_reciprocal_sqrt, bias=one[:])
 
             def first_product():
-                nc.vector.tensor_tensor(part, num[:, cols], root, MULT)
+                if unit < SQUARED_UNITS:
+                    nc.scalar.activation(out=part, in_=root, func=ACT.Square)
+                else:
+                    nc.vector.tensor_tensor(part, num[:, cols], root, MULT)
 
             def second_product():
-                nc.vector.tensor_tensor(result[:, cols], part, root, MULT)
+                other = num[:, cols] if unit < SQUARED_UNITS else root
+                nc.vector.tensor_tensor(result[:, cols], other, part, MULT)
                 rows = out[tiles[0] * P : (tiles[-1] + 1) * P, CHUNKS[c][0] : CHUNKS[c][1]]
                 nc.sync.dma_start(
                     out=rows.rearrange("(t p) m -> p t m", p=P),
@@ -314,17 +325,16 @@ def tile_list_hive_diary_kernel(
             return [sums, inverse_root, first_product, second_product]
 
         out_tiles = N // P
-        bank_pairs = [(banks[6], banks[7]), (banks[0], banks[1])]
         units = []
         for c in range(len(CHUNKS) - 1):
             group = BANK // widths[c]
             for tile in range(0, out_tiles, group):
-                units.append((c, list(range(tile, tile + group)), *bank_pairs[len(units) % 2]))
-        for tile, pair in enumerate([(banks[2], banks[4]), (banks[3], banks[5])] + bank_pairs):
+                units.append((c, list(range(tile, tile + group)), banks[5 + len(units) % 2], (banks[7], banks[0], banks[1])[len(units) % 3]))
+        for tile, pair in enumerate([(banks[n], banks[m]) for n, m in ((2, 3), (5, 7), (6, 4), (0, 1))]):
             units.append((len(CHUNKS) - 1, [tile], *pair))
         steps = [score_steps(unit, *what) for unit, what in enumerate(units)]
         queue = [
-            steps[n - k][k] for n in range(len(units) + 3) for k in (2, 3, 1, 0) if 0 <= n - k < len(units)
+            steps[n - k][k] for n in range(len(units) + 3) for k in (3, 2, 1, 0) if 0 <= n - k < len(units)
         ]
 
         turns = len(CHUNKS) * ROW_TILES
@@ -336,8 +346,9 @@ def tile_list_hive_diary_kernel(
             c, i = divmod(turn - QUANTISE_LAG, ROW_TILES)
             if c >= 0 and i % PACK == PACK - 1:
                 quantise_z(c, i // PACK)
-            elif FIRST_SCORE_TURN <= turn < turns:
-                queue[0]()
-                queue = queue[1:]
+            if FIRST_SCORE_TURN <= turn < turns:
+                for step in queue[0:STEPS_A_TURN]:
+                    step()
+                queue = queue[STEPS_A_TURN:]
         for step in queue:
             step()

@@ -25,6 +25,7 @@ BANK = 512
 QUADRANTS = 4
 LIST_ROWS = 16
 ROW_TILES = H // P
+QUARTER = S // 4
 HALF = S // 2
 W_COLS = 256
 CHUNKS = [(0, 512), (512, 768), (768, 1024)]
@@ -73,6 +74,7 @@ def tile_list_hive_diary_kernel(
 
         rooms = [held(f"room{c}", [P, PASSES * PACK * W_COLS], F32) for c in range(H // W_COLS)]
         casts = [held(f"cast{n}", [P, S], F32) for n in range(2)]
+        second_room, second_cast = held("second_room", [P, S], F32), held("second_cast", [P, HALF], F32)
         low, high = slice(0, S), slice(S, 2 * S)
         h_bufs = {
             i: rooms[(i + 1) // 2 % len(rooms)][:, high] if i % 2 == 1 else rooms[i // 2 - 1][:, low]
@@ -89,30 +91,31 @@ def tile_list_hive_diary_kernel(
         def load_page(i):
             nc.sync.dma_start(out=pages[i][:], in_=page0[i * P : (i + 1) * P, :])
 
-        def load_weight(w, c, room):
-            size = PACK * W_COLS
+        def load_weight(w, first, width, room):
+            size = PACK * width
             raws = [room[:, a * size : (a + 1) * size].rearrange("p (j c) -> p j c", j=PACK) for a in range(PASSES)]
             for a in range(PASSES):
-                rows = w[a * K_PASS : (a + 1) * K_PASS, c * W_COLS : (c + 1) * W_COLS]
+                rows = w[a * K_PASS : (a + 1) * K_PASS, first : first + width]
                 nc.sync.dma_start(out=raws[a], in_=rows.rearrange("(p j) c -> p j c", j=PACK))
             return raws
 
         def quantise_weight(name, raws, cast):
-            size = PACK * W_COLS
+            width = raws[0].shape[2]
+            size = PACK * width
             grouped = cast[:].bitcast(BF16)[:, 0 : PASSES * size]
             for a in range(PASSES):
                 nc.scalar.copy(
                     out=grouped[:, a * size : (a + 1) * size].rearrange("p (c i j) -> p c j i", i=4, j=PACK),
                     in_=raws[a].rearrange("p j (c i) -> p c j i", i=4),
                 )
-            codes = held(f"{name}_codes", [P, PASSES * W_COLS], U32)
-            scales = held(f"{name}_scales", [P, PASSES * W_COLS], U8)
+            codes = held(f"{name}_codes", [P, PASSES * width], U32)
+            scales = held(f"{name}_scales", [P, PASSES * width], U8)
             nc.vector.quantize_mx(out=codes[:].bitcast(FP8X4), scales=scales[:], in_=grouped)
-            return codes, scales
+            return [(codes, scales, width, first) for first in range(0, width, P)]
 
         def stationary(weight_mx, tile, a):
-            codes, scales = weight_mx[tile * P // W_COLS]
-            first = a * W_COLS + tile * P % W_COLS
+            codes, scales, width, first = weight_mx[tile]
+            first = a * width + first
             return codes[:, first : first + P].bitcast(FP8X4), scales[:, first : first + P]
 
         nc.gpsimd.memset(planes[:].bitcast(I32), 0)
@@ -120,19 +123,21 @@ def tile_list_hive_diary_kernel(
         warm = held("warm", [P, 1], F32)
         nc.scalar.activation(out=warm[:], in_=one[:], func=ACT.Abs_reciprocal_sqrt, bias=one[:])
         nc.sync.dma_start(tab_list[:], offs)
+        nc.sync.dma_start(put_list[:], offs2)
         for q in range(QUADRANTS):
             nc.sync.dma_start(
                 out=planes[32 * q : 32 * q + 4 * PASSES, :].bitcast(I32),
                 in_=tab_scales[:, 4 * q : 4 * q + 4, :].bitcast(I32),
             )
         load_words(0)
-        w1_raw = [load_weight(w1, 0, rooms[0])]
+        w1_raw = [load_weight(w1, 0, P, rooms[0])]
         load_words(1)
-        nc.sync.dma_start(out=wgs_sb[:], in_=wgs)
-        nc.sync.dma_start(put_list[:], offs2)
+        nc.sync.dma_start(out=wgs_sb[:, 0:HALF], in_=wgs[:, 0:HALF])
         load_page(0)
+        second_raw = load_weight(w1, P, P, second_room)
+        nc.sync.dma_start(out=wgs_sb[:, HALF:S], in_=wgs[:, HALF:S])
         for c in range(1, len(rooms)):
-            w1_raw.append(load_weight(w1, c, rooms[c]))
+            w1_raw.append(load_weight(w1, c * W_COLS, W_COLS, rooms[c]))
             load_page(c)
         load_page(4)
         load_page(5)
@@ -151,9 +156,9 @@ def tile_list_hive_diary_kernel(
             )
         make_identity(nc, ident[:])
 
-        def pick_words(a, hf):
-            picks = entries(tab_list, hf * HALF, (hf + 1) * HALF)
-            nc.vector.tensor_copy(picked_words[a][hf][:], words[a][:].indirect(picks))
+        def pick_words(a, hf, first=0, end=HALF):
+            picks = entries(tab_list, hf * HALF + first, hf * HALF + end)
+            nc.vector.tensor_copy(picked_words[a][hf][:, first:end], words[a][:].indirect(picks))
 
         def pick_planes(hf):
             picks = entries(tab_list, hf * HALF, (hf + 1) * HALF)
@@ -161,45 +166,50 @@ def tile_list_hive_diary_kernel(
 
         pick_planes(0)
         pick_words(0, 0)
-        pick_words(1, 0)
-        w1_mx = [quantise_weight("w1_0", w1_raw[0], casts[0])]
+        pick_words(1, 0, 0, QUARTER)
+        pick_words(1, 0, QUARTER, HALF)
+        w1_mx = quantise_weight("w1_0", w1_raw[0], casts[0])
         pick_planes(1)
         pick_words(0, 1)
         pick_words(1, 1)
+        w1_mx = w1_mx + quantise_weight("w1_second", second_raw, second_cast)
 
         def write_entries(i):
             if i == 0:
                 halves = [casts[1 - hf][:, HALF // 2 : HALF // 2 + HALF] for hf in range(2)]
-                pieces = [(halves[hf], hf * HALF, (hf + 1) * HALF) for hf in range(2)]
+                halves[1] = second_room[:, 0:HALF]
+                sums = [(0, 0, QUARTER, banks[0]), (0, QUARTER, HALF, banks[2]), (1, 0, HALF, banks[1])]
+                pieces = [(halves[hf][:, lo:hi], hf * HALF + lo, hf * HALF + hi) for hf, lo, hi, bank in sums]
             else:
                 halves = [h_bufs[i][:, hf * HALF : (hf + 1) * HALF] for hf in range(2)]
+                sums = [(hf, 0, HALF, h_banks[hf]) for hf in range(2)]
                 pieces = [(h_bufs[i], 0, S)]
-            for hf in range(2):
+            for hf, lo, hi, bank in sums:
                 for a in range(PASSES):
                     codes, scales = stationary(w1_mx, i, a)
                     nc.tensor.matmul_mx(
-                        out=h_banks[hf][:],
+                        out=bank[:, lo:hi],
                         lhsT=codes,
                         lhsT_scale=scales,
-                        rhs=picked_words[a][hf][:].bitcast(FP8X4),
-                        rhs_scale=picked_planes[hf][4 * a : P, :],
+                        rhs=picked_words[a][hf][:, lo:hi].bitcast(FP8X4),
+                        rhs_scale=picked_planes[hf][4 * a : P, lo:hi],
                         start=(a == 0),
                         stop=(a == PASSES - 1),
                     )
-                nc.scalar.copy(out=halves[hf], in_=h_banks[hf][:])
+                nc.scalar.copy(out=halves[hf][:, lo:hi], in_=bank[:, lo:hi])
             for h, first, end in pieces:
                 days = pages[i][:].indirect(entries(put_list, first, end))
                 nc.vector.tensor_tensor(days, h, wgs_sb[:, first:end], MULT)
 
         w3_mx = []
         for i in range(ROW_TILES):
-            if i % 2 == 1 and len(w1_mx) < len(rooms):
-                c = len(w1_mx)
-                w1_mx.append(quantise_weight(f"w1_{c}", w1_raw[c], casts[c % 2]))
+            if i % 2 == 1 and i + 1 < ROW_TILES:
+                c = (i + 1) // 2
+                w1_mx = w1_mx + quantise_weight(f"w1_{c}", w1_raw[c], casts[c % 2])
             write_entries(i)
             if i in (4, 5):
                 c = i - 4
-                w3_mx.append(quantise_weight(f"w3_{c}", load_weight(w3, c, rooms[1 + 2 * c]), casts[c]))
+                w3_mx = w3_mx + quantise_weight(f"w3_{c}", load_weight(w3, c * W_COLS, W_COLS, rooms[1 + 2 * c]), casts[c])
 
         nc.tensor.transpose(h_banks[1][:, 0:P], lam_rows[:], ident[:])
         nc.scalar.copy(out=lam_cols[:], in_=h_banks[1][:, 0:ROW_TILES])

@@ -29,14 +29,15 @@ QUARTER = S // 4
 HALF = S // 2
 W_COLS = 256
 CHUNKS = [(0, 512), (512, 768), (768, 1024)]
-SUM_BANKS = 2
+GROUP = 256
+SUM_BANKS = 3
 COLLECT_LAG = 1
 QUANTISE_LAG = 1
 FIRST_SCORE_TURN = 12
 SCORE_SLOTS = 4
-STEPS_A_TURN = 1
 RING = 3
-SQUARED_UNITS = 4
+DEFERRED = (1, 2)
+SQUARED_UNITS = 3
 RESULT_BUFS = 6
 
 
@@ -82,7 +83,7 @@ def tile_list_hive_diary_kernel(
         }
 
         banks = [psum.tile([P, BANK], F32, name=f"bank{b}") for b in range(8)]
-        h_banks, sum_banks, word_banks = banks[0:2], banks[2 : 2 + SUM_BANKS], banks[4:5]
+        h_banks, sum_banks, word_banks = banks[0:2], [banks[2], banks[3], banks[1]][0:SUM_BANKS], banks[4:5]
 
         def load_words(a):
             source = tab_words[a].rearrange("p t i -> p (t i)").bitcast(I32)
@@ -220,8 +221,9 @@ def tile_list_hive_diary_kernel(
 
         widths = [end - first for first, end in CHUNKS]
         z_rows = [held(f"z_rows{b}", [P, PACK * BANK], BF16) for b in range(PASSES)]
-        z_codes = [[held(f"z_codes{c}_{b}", [P, w], U32) for b in range(PASSES)] for c, w in enumerate(widths)]
-        z_scales = [[held(f"z_scales{c}_{b}", [P, w], U8) for b in range(PASSES)] for c, w in enumerate(widths)]
+        groups = TREATMENTS // GROUP
+        z_codes = [[held(f"z_codes{g}_{b}", [P, GROUP], U32) for b in range(PASSES)] for g in range(groups)]
+        z_scales = [[held(f"z_scales{g}_{b}", [P, GROUP], U8) for b in range(PASSES)] for g in range(groups)]
         visits = [h_bufs[ROW_TILES - 1], wgs_sb]
 
         def fetch(turn):
@@ -256,19 +258,20 @@ def tile_list_hive_diary_kernel(
         def quantise_z(c, b):
             blocks = widths[c] // P
             pairs = z_rows[b][:, 0 : PACK * widths[c]].bitcast(F32)
-            grouped = stage.tile([P, widths[c] * PACK], BF16, name="z_grouped", tag="z_grouped", align_bytes=64)
             for j0 in range(0, blocks, 2):
-                word_bank = word_banks[(j0 // 2 + b) % len(word_banks)]
+                g = (CHUNKS[c][0] + j0 * P) // GROUP
+                grouped = stage.tile([P, GROUP * PACK], BF16, name="z_grouped", tag="z_grouped", bufs=3, align_bytes=64)
+                word_bank = word_banks[0]
                 for j in range(2):
                     for u in range(2):
                         source, target = (u * blocks + j0 + j) * P, (2 * j + u) * P
                         nc.tensor.transpose(word_bank[:, target : target + P], pairs[:, source : source + P], ident[:])
-                grouped_words = grouped[:].bitcast(F32)[:, j0 * 2 * P : (j0 + 2) * 2 * P]
+                grouped_words = grouped[:].bitcast(F32)
                 nc.scalar.copy(
                     out=grouped_words.rearrange("p (j m u) -> p j m u", j=2, u=2),
                     in_=word_bank[:].rearrange("p (j u m) -> p j m u", j=2, u=2),
                 )
-            nc.vector.quantize_mx(out=z_codes[c][b][:].bitcast(FP8X4), scales=z_scales[c][b][:], in_=grouped[:])
+                nc.vector.quantize_mx(out=z_codes[g][b][:].bitcast(FP8X4), scales=z_scales[g][b][:], in_=grouped[:])
 
         def den_sums(c, tile, target):
             for b in range(PASSES):
@@ -284,8 +287,8 @@ def tile_list_hive_diary_kernel(
                 )
 
         def num_sums(c, tile, target):
-            step = widths[c]
-            for first in range(0, widths[c], step):
+            step = GROUP
+            for first in range(0, GROUP, step):
                 cols = slice(first, first + step)
                 for b in range(PASSES):
                     nc.tensor.matmul_mx(
@@ -299,34 +302,42 @@ def tile_list_hive_diary_kernel(
                     )
 
         def score_steps(unit, c, tiles, den, num):
-            width = widths[c]
+            width = GROUP
             cols = slice(0, len(tiles) * width)
             slot = (unit % SCORE_SLOTS) * BANK
             size = casts[unit % 2][:, cols]
             root = rooms[1][:, slot : slot + BANK][:, cols]
             part = rooms[3][:, slot : slot + BANK][:, cols]
-            result = stage.tile([P, BANK], F32, name="result", tag="result", bufs=RESULT_BUFS)
+
+            def numerators():
+                for n, tile in enumerate(tiles):
+                    num_sums(c, tile, num[:, n * width : (n + 1) * width])
 
             def sums():
                 for n, tile in enumerate(tiles):
                     den_sums(c, tile, den[:, n * width : (n + 1) * width])
-                for n, tile in enumerate(tiles):
-                    num_sums(c, tile, num[:, n * width : (n + 1) * width])
+                if c == groups - 1:
+                    numerators()
                 nc.scalar.activation(out=size, in_=den[:, cols], func=ACT.Abs)
 
             def inverse_root():
                 nc.scalar.activation(out=root, in_=size, func=ACT.Abs_reciprocal_sqrt, bias=one[:])
 
             def first_product():
+                if c < groups - 1 and unit not in DEFERRED:
+                    numerators()
                 if unit < SQUARED_UNITS:
                     nc.scalar.activation(out=part, in_=root, func=ACT.Square)
                 else:
                     nc.vector.tensor_tensor(part, num[:, cols], root, MULT)
 
             def second_product():
+                if unit in DEFERRED:
+                    numerators()
+                result = stage.tile([P, BANK], F32, name="result", tag="result", bufs=RESULT_BUFS)
                 other = num[:, cols] if unit < SQUARED_UNITS else root
                 nc.vector.tensor_tensor(result[:, cols], other, part, MULT)
-                rows = out[tiles[0] * P : (tiles[-1] + 1) * P, CHUNKS[c][0] : CHUNKS[c][1]]
+                rows = out[tiles[0] * P : (tiles[-1] + 1) * P, c * GROUP : (c + 1) * GROUP]
                 nc.sync.dma_start(
                     out=rows.rearrange("(t p) m -> p t m", p=P),
                     in_=result[:, cols].rearrange("p (t m) -> p t m", t=len(tiles)),
@@ -336,15 +347,18 @@ def tile_list_hive_diary_kernel(
 
         out_tiles = N // P
         units = []
-        for c in range(len(CHUNKS) - 1):
-            group = BANK // widths[c]
+        for c in range(groups - 1):
+            group = BANK // GROUP
             for tile in range(0, out_tiles, group):
-                units.append((c, list(range(tile, tile + group)), banks[5 + len(units) % 2], (banks[7], banks[0], banks[1])[len(units) % 3]))
-        for tile, pair in enumerate([(banks[n], banks[m]) for n, m in ((2, 3), (5, 7), (6, 4), (0, 1))]):
-            units.append((len(CHUNKS) - 1, [tile], *pair))
+                num = (banks[7], banks[0])[len(units) % 2]
+                if len(units) in DEFERRED:
+                    num = sum_banks[DEFERRED.index(len(units))]
+                units.append((c, list(range(tile, tile + group)), banks[5 + len(units) % 2], num))
+        for tile, pair in enumerate([(banks[n], banks[m]) for n, m in ((1, 4), (5, 2), (6, 3), (1, 7))]):
+            units.append((groups - 1, [tile], *pair))
         steps = [score_steps(unit, *what) for unit, what in enumerate(units)]
         queue = [
-            steps[n - k][k] for n in range(len(units) + 3) for k in (3, 2, 1, 0) if 0 <= n - k < len(units)
+            steps[n - k][k] for n in range(len(units) + 3) for k in (3, 2, 1, 0) if 0 <= n - k < len(units) and not (k == 3 and n - k in DEFERRED)
         ]
 
         turns = len(CHUNKS) * ROW_TILES
@@ -357,8 +371,9 @@ def tile_list_hive_diary_kernel(
             if c >= 0 and i % PACK == PACK - 1:
                 quantise_z(c, i // PACK)
             if FIRST_SCORE_TURN <= turn < turns:
-                for step in queue[0:STEPS_A_TURN]:
+                count = 1 + turn % 2
+                for step in queue[0:count]:
                     step()
-                queue = queue[STEPS_A_TURN:]
-        for step in queue:
+                queue = queue[count:]
+        for step in [steps[unit][3] for unit in DEFERRED] + queue:
             step()

@@ -28,15 +28,13 @@ ROW_TILES = H // P
 QUARTER = S // 4
 HALF = S // 2
 W_COLS = 256
-CHUNKS = [(0, 512), (512, 768), (768, 1024)]
-GROUP = 256
-SUM_BANKS = 3
-COLLECT_LAG = 1
-QUANTISE_LAG = 1
-FIRST_SCORE_TURN = 12
+GROUP = 2 * P
 SCORE_SLOTS = 4
+
+CHUNKS = [(0, 512), (512, 768), (768, 1024)]
 RING = 3
-DEFERRED = (1, 2)
+FIRST_SCORE_TURN = 12
+STEPS = (1, 2)
 SQUARED_UNITS = 3
 RESULT_BUFS = 6
 
@@ -61,8 +59,8 @@ def tile_list_hive_diary_kernel(
         ]
         words = [held(f"words{a}", [P, T], U32) for a in range(PASSES)]
         planes = held("planes", [P, T], U8)
-        picked_words = [[held(f"picked_words{a}_{hf}", [P, HALF], U32) for hf in range(2)] for a in range(PASSES)]
-        picked_planes = [held(f"picked_planes{hf}", [P, HALF], U8) for hf in range(2)]
+        picked_words = [held(f"picked_words{a}", [P, S], U32) for a in range(PASSES)]
+        picked_planes = held("picked_planes", [P, S], U8)
         pages = [held(f"page{i}", [P, T2], F32) for i in range(ROW_TILES)]
         wgs_sb = held("wgs_sb", [P, S], F32)
         lam_rows = held("lam_rows", [P, P], F32)
@@ -83,7 +81,9 @@ def tile_list_hive_diary_kernel(
         }
 
         banks = [psum.tile([P, BANK], F32, name=f"bank{b}") for b in range(8)]
-        h_banks, sum_banks, word_banks = banks[0:2], [banks[2], banks[3], banks[1]][0:SUM_BANKS], banks[4:5]
+        h_banks = banks[0:2]
+        sum_banks, word_bank = [banks[2], banks[3], banks[1]], banks[4]
+        den_banks, num_banks = banks[5:7], [banks[7], banks[0]]
 
         def load_words(a):
             source = tab_words[a].rearrange("p t i -> p (t i)").bitcast(I32)
@@ -133,8 +133,9 @@ def tile_list_hive_diary_kernel(
         load_words(0)
         w1_raw = [load_weight(w1, 0, P, rooms[0])]
         load_words(1)
-        nc.sync.dma_start(out=wgs_sb[:, 0:HALF], in_=wgs[:, 0:HALF])
+        nc.sync.dma_start(out=wgs_sb[:, 0:QUARTER], in_=wgs[:, 0:QUARTER])
         load_page(0)
+        nc.sync.dma_start(out=wgs_sb[:, QUARTER:HALF], in_=wgs[:, QUARTER:HALF])
         second_raw = load_weight(w1, P, P, second_room)
         nc.sync.dma_start(out=wgs_sb[:, HALF:S], in_=wgs[:, HALF:S])
         for c in range(1, len(rooms)):
@@ -157,28 +158,19 @@ def tile_list_hive_diary_kernel(
             )
         make_identity(nc, ident[:])
 
-        def pick_words(a, hf, first=0, end=HALF):
-            picks = entries(tab_list, hf * HALF + first, hf * HALF + end)
-            nc.vector.tensor_copy(picked_words[a][hf][:, first:end], words[a][:].indirect(picks))
+        def pick(picked, table, first, end):
+            nc.vector.tensor_copy(picked[:, first:end], table[:].indirect(entries(tab_list, first, end)))
 
-        def pick_planes(hf):
-            picks = entries(tab_list, hf * HALF, (hf + 1) * HALF)
-            nc.vector.tensor_copy(picked_planes[hf][:], planes[:].indirect(picks))
-
-        pick_planes(0)
-        pick_words(0, 0)
-        pick_words(1, 0, 0, QUARTER)
-        pick_words(1, 0, QUARTER, HALF)
+        pick(picked_planes, planes, 0, S)
+        pick(picked_words[0], words[0], 0, S)
+        pick(picked_words[1], words[1], 0, QUARTER)
         w1_mx = quantise_weight("w1_0", w1_raw[0], casts[0])
-        pick_planes(1)
-        pick_words(0, 1)
-        pick_words(1, 1)
+        pick(picked_words[1], words[1], QUARTER, S)
         w1_mx = w1_mx + quantise_weight("w1_second", second_raw, second_cast)
 
         def write_entries(i):
             if i == 0:
-                halves = [casts[1 - hf][:, HALF // 2 : HALF // 2 + HALF] for hf in range(2)]
-                halves[1] = second_room[:, 0:HALF]
+                halves = [casts[1][:, QUARTER : QUARTER + HALF], second_room[:, 0:HALF]]
                 sums = [(0, 0, QUARTER, banks[0]), (0, QUARTER, HALF, banks[2]), (1, 0, HALF, banks[1])]
                 pieces = [(halves[hf][:, lo:hi], hf * HALF + lo, hf * HALF + hi) for hf, lo, hi, bank in sums]
             else:
@@ -192,8 +184,8 @@ def tile_list_hive_diary_kernel(
                         out=bank[:, lo:hi],
                         lhsT=codes,
                         lhsT_scale=scales,
-                        rhs=picked_words[a][hf][:, lo:hi].bitcast(FP8X4),
-                        rhs_scale=picked_planes[hf][4 * a : P, lo:hi],
+                        rhs=picked_words[a][:, hf * HALF + lo : hf * HALF + hi].bitcast(FP8X4),
+                        rhs_scale=picked_planes[4 * a : P, hf * HALF + lo : hf * HALF + hi],
                         start=(a == 0),
                         stop=(a == PASSES - 1),
                     )
@@ -210,7 +202,8 @@ def tile_list_hive_diary_kernel(
             write_entries(i)
             if i in (4, 5):
                 c = i - 4
-                w3_mx = w3_mx + quantise_weight(f"w3_{c}", load_weight(w3, c * W_COLS, W_COLS, rooms[1 + 2 * c]), casts[c])
+                raws = load_weight(w3, c * W_COLS, W_COLS, rooms[1 + 2 * c])
+                w3_mx = w3_mx + quantise_weight(f"w3_{c}", raws, casts[c])
 
         nc.tensor.transpose(h_banks[1][:, 0:P], lam_rows[:], ident[:])
         nc.scalar.copy(out=lam_cols[:], in_=h_banks[1][:, 0:ROW_TILES])
@@ -220,8 +213,8 @@ def tile_list_hive_diary_kernel(
             nc.scalar.copy(out=weights[1][i][:], in_=spread)
 
         widths = [end - first for first, end in CHUNKS]
+        turns, groups = len(CHUNKS) * ROW_TILES, TREATMENTS // GROUP
         z_rows = [held(f"z_rows{b}", [P, PACK * BANK], BF16) for b in range(PASSES)]
-        groups = TREATMENTS // GROUP
         z_codes = [[held(f"z_codes{g}_{b}", [P, GROUP], U32) for b in range(PASSES)] for g in range(groups)]
         z_scales = [[held(f"z_scales{g}_{b}", [P, GROUP], U8) for b in range(PASSES)] for g in range(groups)]
         visits = [h_bufs[ROW_TILES - 1], wgs_sb]
@@ -230,16 +223,16 @@ def tile_list_hive_diary_kernel(
             c, i = divmod(turn, ROW_TILES)
             width = widths[c]
             piece, which = divmod(turn % min(RING, S // width), 2)
-            scaled = visits[which][:, piece * 2 * width : (piece + 1) * 2 * width]
-            bank = sum_banks[turn % SUM_BANKS]
+            weighed = visits[which][:, piece * 2 * width : (piece + 1) * 2 * width]
+            bank = sum_banks[turn % len(sum_banks)]
             for n, days in enumerate((before_list, after_list)):
                 visit = pages[i][:].indirect(entries(days, *CHUNKS[c]))
-                nc.vector.tensor_tensor(scaled[:, n * width : (n + 1) * width], visit, weights[n][i][:, 0:width], MULT)
+                nc.vector.tensor_tensor(weighed[:, n * width : (n + 1) * width], visit, weights[n][i][:, 0:width], MULT)
             for j in range(width // P):
                 for n in (1, 0):
                     nc.tensor.matmul(
                         bank[:, j * P : (j + 1) * P],
-                        scaled[:, n * width + j * P : n * width + (j + 1) * P],
+                        weighed[:, n * width + j * P : n * width + (j + 1) * P],
                         ident[:],
                         is_transpose=True,
                         start=(n == 1),
@@ -250,9 +243,10 @@ def tile_list_hive_diary_kernel(
             c, i = divmod(turn, ROW_TILES)
             b, quarter = divmod(i, PACK)
             rows = z_rows[b][:, 0 : PACK * widths[c]].rearrange("m (u j p e) -> m u j p e", u=2, p=P, e=2)
+            sums = sum_banks[turn % len(sum_banks)][:, 0 : widths[c]]
             nc.scalar.copy(
                 out=rows[:, :, :, 32 * quarter : 32 * (quarter + 1), :],
-                in_=sum_banks[turn % SUM_BANKS][:, 0 : widths[c]].rearrange("m (j p u e) -> m u j p e", p=32, u=2, e=2),
+                in_=sums.rearrange("m (j p u e) -> m u j p e", p=32, u=2, e=2),
             )
 
         def quantise_z(c, b):
@@ -261,119 +255,106 @@ def tile_list_hive_diary_kernel(
             for j0 in range(0, blocks, 2):
                 g = (CHUNKS[c][0] + j0 * P) // GROUP
                 grouped = stage.tile([P, GROUP * PACK], BF16, name="z_grouped", tag="z_grouped", bufs=3, align_bytes=64)
-                word_bank = word_banks[0]
                 for j in range(2):
                     for u in range(2):
                         source, target = (u * blocks + j0 + j) * P, (2 * j + u) * P
                         nc.tensor.transpose(word_bank[:, target : target + P], pairs[:, source : source + P], ident[:])
-                grouped_words = grouped[:].bitcast(F32)
                 nc.scalar.copy(
-                    out=grouped_words.rearrange("p (j m u) -> p j m u", j=2, u=2),
+                    out=grouped[:].bitcast(F32).rearrange("p (j m u) -> p j m u", j=2, u=2),
                     in_=word_bank[:].rearrange("p (j u m) -> p j m u", j=2, u=2),
                 )
                 nc.vector.quantize_mx(out=z_codes[g][b][:].bitcast(FP8X4), scales=z_scales[g][b][:], in_=grouped[:])
 
-        def den_sums(c, tile, target):
-            for b in range(PASSES):
-                codes, scales = stationary(w3_mx, tile, b)
-                nc.tensor.matmul_mx(
-                    out=target,
-                    lhsT=codes,
-                    lhsT_scale=scales,
-                    rhs=z_codes[c][b][:].bitcast(FP8X4),
-                    rhs_scale=z_scales[c][b][:],
-                    start=(b == 0),
-                    stop=(b == PASSES - 1),
-                )
+        def den_operand(tile, b):
+            return stationary(w3_mx, tile, b)
 
-        def num_sums(c, tile, target):
-            step = GROUP
-            for first in range(0, GROUP, step):
-                cols = slice(first, first + step)
+        def num_operand(tile, b):
+            codes = w2_codes[:, b, 2 * tile * P : 2 * (tile + 1) * P].bitcast(FP4X4)
+            return codes, w2_planes[:, b, tile * P : (tile + 1) * P]
+
+        def bank_sums(operand, g, tiles, bank):
+            for n, tile in enumerate(tiles):
                 for b in range(PASSES):
+                    codes, scales = operand(tile, b)
                     nc.tensor.matmul_mx(
-                        out=target[:, cols],
-                        lhsT=w2_codes[:, b, 2 * tile * P : 2 * (tile + 1) * P].bitcast(FP4X4),
-                        lhsT_scale=w2_planes[:, b, tile * P : (tile + 1) * P],
-                        rhs=z_codes[c][b][:, cols].bitcast(FP8X4),
-                        rhs_scale=z_scales[c][b][:, cols],
+                        out=bank[:, n * GROUP : (n + 1) * GROUP],
+                        lhsT=codes,
+                        lhsT_scale=scales,
+                        rhs=z_codes[g][b][:].bitcast(FP8X4),
+                        rhs_scale=z_scales[g][b][:],
                         start=(b == 0),
                         stop=(b == PASSES - 1),
                     )
 
-        def score_steps(unit, c, tiles, den, num):
-            width = GROUP
-            cols = slice(0, len(tiles) * width)
+        held_back = list(range(1, SQUARED_UNITS))
+
+        def score_steps(unit, g, tiles, den, num):
+            cols = slice(0, len(tiles) * GROUP)
             slot = (unit % SCORE_SLOTS) * BANK
             size = casts[unit % 2][:, cols]
             root = rooms[1][:, slot : slot + BANK][:, cols]
             part = rooms[3][:, slot : slot + BANK][:, cols]
+            squared = unit < SQUARED_UNITS
+            num_step = 0 if g == groups - 1 else 3 if unit in held_back else 2
 
-            def numerators():
-                for n, tile in enumerate(tiles):
-                    num_sums(c, tile, num[:, n * width : (n + 1) * width])
-
-            def sums():
-                for n, tile in enumerate(tiles):
-                    den_sums(c, tile, den[:, n * width : (n + 1) * width])
-                if c == groups - 1:
-                    numerators()
+            def absolute():
+                bank_sums(den_operand, g, tiles, den)
+                if num_step == 0:
+                    bank_sums(num_operand, g, tiles, num)
                 nc.scalar.activation(out=size, in_=den[:, cols], func=ACT.Abs)
 
             def inverse_root():
                 nc.scalar.activation(out=root, in_=size, func=ACT.Abs_reciprocal_sqrt, bias=one[:])
 
             def first_product():
-                if c < groups - 1 and unit not in DEFERRED:
-                    numerators()
-                if unit < SQUARED_UNITS:
+                if num_step == 2:
+                    bank_sums(num_operand, g, tiles, num)
+                if squared:
                     nc.scalar.activation(out=part, in_=root, func=ACT.Square)
                 else:
                     nc.vector.tensor_tensor(part, num[:, cols], root, MULT)
 
-            def second_product():
-                if unit in DEFERRED:
-                    numerators()
+            def last_product():
+                if num_step == 3:
+                    bank_sums(num_operand, g, tiles, num)
                 result = stage.tile([P, BANK], F32, name="result", tag="result", bufs=RESULT_BUFS)
-                other = num[:, cols] if unit < SQUARED_UNITS else root
-                nc.vector.tensor_tensor(result[:, cols], other, part, MULT)
-                rows = out[tiles[0] * P : (tiles[-1] + 1) * P, c * GROUP : (c + 1) * GROUP]
+                nc.vector.tensor_tensor(result[:, cols], num[:, cols] if squared else root, part, MULT)
+                rows = out[tiles[0] * P : (tiles[-1] + 1) * P, g * GROUP : (g + 1) * GROUP]
                 nc.sync.dma_start(
                     out=rows.rearrange("(t p) m -> p t m", p=P),
                     in_=result[:, cols].rearrange("p (t m) -> p t m", t=len(tiles)),
                 )
 
-            return [sums, inverse_root, first_product, second_product]
+            return [absolute, inverse_root, first_product, last_product]
 
-        out_tiles = N // P
         units = []
-        for c in range(groups - 1):
-            group = BANK // GROUP
-            for tile in range(0, out_tiles, group):
-                num = (banks[7], banks[0])[len(units) % 2]
-                if len(units) in DEFERRED:
-                    num = sum_banks[DEFERRED.index(len(units))]
-                units.append((c, list(range(tile, tile + group)), banks[5 + len(units) % 2], num))
-        for tile, pair in enumerate([(banks[n], banks[m]) for n, m in ((1, 4), (5, 2), (6, 3), (1, 7))]):
-            units.append((groups - 1, [tile], *pair))
+        for unit in range(2 * (groups - 1)):
+            g, pair = divmod(unit, 2)
+            num = sum_banks[held_back.index(unit)] if unit in held_back else num_banks[unit % 2]
+            units.append((g, [2 * pair, 2 * pair + 1], den_banks[unit % 2], num))
+        last_dens = [sum_banks[2], den_banks[0], den_banks[1], sum_banks[2]]
+        last_nums = [word_bank, sum_banks[0], sum_banks[1], num_banks[0]]
+        for tile in range(N // P):
+            units.append((groups - 1, [tile], last_dens[tile], last_nums[tile]))
         steps = [score_steps(unit, *what) for unit, what in enumerate(units)]
         queue = [
-            steps[n - k][k] for n in range(len(units) + 3) for k in (3, 2, 1, 0) if 0 <= n - k < len(units) and not (k == 3 and n - k in DEFERRED)
+            steps[n - k][k]
+            for n in range(len(units) + 3)
+            for k in (3, 2, 1, 0)
+            if 0 <= n - k < len(units) and not (k == 3 and n - k in held_back)
         ]
 
-        turns = len(CHUNKS) * ROW_TILES
-        for turn in range(turns + QUANTISE_LAG):
+        for turn in range(turns + 1):
             if turn < turns:
                 fetch(turn)
-            if 0 <= turn - COLLECT_LAG < turns:
-                collect(turn - COLLECT_LAG)
-            c, i = divmod(turn - QUANTISE_LAG, ROW_TILES)
-            if c >= 0 and i % PACK == PACK - 1:
-                quantise_z(c, i // PACK)
+            if turn >= 1:
+                collect(turn - 1)
+                c, i = divmod(turn - 1, ROW_TILES)
+                if i % PACK == PACK - 1:
+                    quantise_z(c, i // PACK)
             if FIRST_SCORE_TURN <= turn < turns:
-                count = 1 + turn % 2
-                for step in queue[0:count]:
+                for step in queue[0 : STEPS[turn % 2]]:
                     step()
-                queue = queue[count:]
-        for step in [steps[unit][3] for unit in DEFERRED] + queue:
+                queue = queue[STEPS[turn % 2] :]
+        for step in [steps[unit][3] for unit in held_back] + queue:
             step()

@@ -26,6 +26,7 @@ QUADRANTS = 4
 LIST_ROWS = 16
 ROW_TILES = H // P
 QUARTER = S // 4
+FIRST = 384
 HALF = S // 2
 W_COLS = 256
 GROUP = 2 * P
@@ -73,7 +74,8 @@ def tile_list_hive_diary_kernel(
 
         rooms = [held(f"room{c}", [P, PASSES * PACK * W_COLS], F32) for c in range(H // W_COLS)]
         casts = [held(f"cast{n}", [P, S], F32) for n in range(2)]
-        second_room, second_cast = held("second_room", [P, S], F32), held("second_cast", [P, HALF], F32)
+        second_space, second_cast = held("second_space", [P, HALF + S], F32), held("second_cast", [P, HALF], F32)
+        second_room = second_space[:, HALF : HALF + S]
         low, high = slice(0, S), slice(S, 2 * S)
         h_bufs = {
             i: rooms[(i + 1) // 2 % len(rooms)][:, high] if i % 2 == 1 else rooms[i // 2 - 1][:, low]
@@ -133,11 +135,10 @@ def tile_list_hive_diary_kernel(
         load_words(0)
         w1_raw = [load_weight(w1, 0, P, rooms[0])]
         load_words(1)
-        nc.sync.dma_start(out=wgs_sb[:, 0:QUARTER], in_=wgs[:, 0:QUARTER])
+        nc.sync.dma_start(out=wgs_sb[:, 0:FIRST], in_=wgs[:, 0:FIRST])
         load_page(0)
-        nc.sync.dma_start(out=wgs_sb[:, QUARTER:HALF], in_=wgs[:, QUARTER:HALF])
         second_raw = load_weight(w1, P, P, second_room)
-        nc.sync.dma_start(out=wgs_sb[:, HALF:S], in_=wgs[:, HALF:S])
+        nc.sync.dma_start(out=wgs_sb[:, FIRST:S], in_=wgs[:, FIRST:S])
         for c in range(1, len(rooms)):
             w1_raw.append(load_weight(w1, c * W_COLS, W_COLS, rooms[c]))
             load_page(c)
@@ -163,33 +164,37 @@ def tile_list_hive_diary_kernel(
 
         pick(picked_planes, planes, 0, S)
         pick(picked_words[0], words[0], 0, S)
-        pick(picked_words[1], words[1], 0, QUARTER)
+        pick(picked_words[1], words[1], 0, FIRST)
         w1_mx = quantise_weight("w1_0", w1_raw[0], casts[0])
-        pick(picked_words[1], words[1], QUARTER, S)
+        pick(picked_words[1], words[1], FIRST, S)
         w1_mx = w1_mx + quantise_weight("w1_second", second_raw, second_cast)
 
         def write_entries(i):
             if i == 0:
-                halves = [casts[1][:, QUARTER : QUARTER + HALF], second_room[:, 0:HALF]]
-                sums = [(0, 0, QUARTER, banks[0]), (0, QUARTER, HALF, banks[2]), (1, 0, HALF, banks[1])]
-                pieces = [(halves[hf][:, lo:hi], hf * HALF + lo, hf * HALF + hi) for hf, lo, hi, bank in sums]
+                first, rest = casts[1][:, HALF : HALF + FIRST], second_space[:, 0 : S - FIRST]
+                sums = [(0, QUARTER, banks[0]), (QUARTER, FIRST, banks[2]), (FIRST, HALF, banks[3]), (HALF, S, banks[1])]
+                copies = [[(first[:, 0:QUARTER], 0, QUARTER)], [(first[:, QUARTER:FIRST], QUARTER, FIRST)]]
+                copies.append([(rest[:, 0 : HALF - FIRST], FIRST, HALF)])
+                copies.append([(rest[:, HALF - FIRST : HALF], HALF, HALF + FIRST), (rest[:, HALF : S - FIRST], HALF + FIRST, S)])
+                pieces = [(first, 0, FIRST), (rest, FIRST, S)]
             else:
-                halves = [h_bufs[i][:, hf * HALF : (hf + 1) * HALF] for hf in range(2)]
-                sums = [(hf, 0, HALF, h_banks[hf]) for hf in range(2)]
+                sums = [(hf * HALF, (hf + 1) * HALF, h_banks[hf]) for hf in range(2)]
+                copies = [[(h_bufs[i][:, lo:hi], lo, hi)] for lo, hi, bank in sums]
                 pieces = [(h_bufs[i], 0, S)]
-            for hf, lo, hi, bank in sums:
+            for (lo, hi, bank), targets in zip(sums, copies):
                 for a in range(PASSES):
                     codes, scales = stationary(w1_mx, i, a)
                     nc.tensor.matmul_mx(
-                        out=bank[:, lo:hi],
+                        out=bank[:, 0 : hi - lo],
                         lhsT=codes,
                         lhsT_scale=scales,
-                        rhs=picked_words[a][:, hf * HALF + lo : hf * HALF + hi].bitcast(FP8X4),
-                        rhs_scale=picked_planes[4 * a : P, hf * HALF + lo : hf * HALF + hi],
+                        rhs=picked_words[a][:, lo:hi].bitcast(FP8X4),
+                        rhs_scale=picked_planes[4 * a : P, lo:hi],
                         start=(a == 0),
                         stop=(a == PASSES - 1),
                     )
-                nc.scalar.copy(out=halves[hf][:, lo:hi], in_=bank[:, lo:hi])
+                for target, first, end in targets:
+                    nc.scalar.copy(out=target, in_=bank[:, first - lo : end - lo])
             for h, first, end in pieces:
                 days = pages[i][:].indirect(entries(put_list, first, end))
                 nc.vector.tensor_tensor(days, h, wgs_sb[:, first:end], MULT)
@@ -294,7 +299,7 @@ def tile_list_hive_diary_kernel(
             size = casts[unit % 2][:, cols]
             root = rooms[1][:, slot : slot + BANK][:, cols]
             part = rooms[3][:, slot : slot + BANK][:, cols]
-            squared = unit < SQUARED_UNITS
+            squared = unit < SQUARED_UNITS or unit == 8
             num_step = 0 if g == groups - 1 else 3 if unit in held_back else 2
 
             def absolute():

@@ -124,7 +124,7 @@ def tile_list_hive_diary_kernel(
         nc.gpsimd.memset(planes[:].bitcast(I32), 0)
         nc.gpsimd.memset(one[:], 1.0)
         warm = held("warm", [P, 1], F32)
-        nc.scalar.activation(out=warm[:], in_=one[:], func=ACT.Abs_reciprocal_sqrt, bias=one[:])
+        nc.scalar.activation(out=warm[:], in_=one[:], func=ACT.Abs_reciprocal_sqrt, bias=1.0)
         nc.sync.dma_start(tab_list[:], offs)
         nc.sync.dma_start(put_list[:], offs2)
         for q in range(QUADRANTS):
@@ -300,16 +300,14 @@ def tile_list_hive_diary_kernel(
             root = rooms[1][:, slot : slot + BANK][:, cols]
             part = rooms[3][:, slot : slot + BANK][:, cols]
             squared = unit < SQUARED_UNITS or unit == 8
-            num_step = 0 if g == groups - 1 else 3 if unit in held_back else 2
+            num_step = 3 if unit in held_back else 2
 
             def absolute():
                 bank_sums(den_operand, g, tiles, den)
-                if num_step == 0:
-                    bank_sums(num_operand, g, tiles, num)
                 nc.scalar.activation(out=size, in_=den[:, cols], func=ACT.Abs)
 
             def inverse_root():
-                nc.scalar.activation(out=root, in_=size, func=ACT.Abs_reciprocal_sqrt, bias=one[:])
+                nc.scalar.activation(out=root, in_=size, func=ACT.Abs_reciprocal_sqrt, bias=1.0)
 
             def first_product():
                 if num_step == 2:

@@ -36,7 +36,7 @@ CHUNKS = [(0, 512), (512, 768), (768, 1024)]
 RING = 3
 FIRST_SCORE_TURN = 12
 STEPS = (1, 2)
-SQUARED_UNITS = 3
+SQUARED_UNITS = (0, 1, 2, 4, 5, 8)
 RESULT_BUFS = 6
 
 
@@ -84,7 +84,7 @@ def tile_list_hive_diary_kernel(
 
         banks = [psum.tile([P, BANK], F32, name=f"bank{b}") for b in range(8)]
         h_banks = banks[0:2]
-        sum_banks, word_bank = [banks[2], banks[3], banks[1]], banks[4]
+        sum_banks, word_bank, waiting_bank = banks[2:4], banks[4], banks[1]
         den_banks, num_banks = banks[5:7], [banks[7], banks[0]]
 
         def load_words(a):
@@ -244,10 +244,14 @@ def tile_list_hive_diary_kernel(
                         stop=(n == 0),
                     )
 
+        def pass_rows(c, b):
+            first = 0 if widths[c] == BANK else P
+            return z_rows[b][:, first : first + PACK * widths[c]]
+
         def collect(turn):
             c, i = divmod(turn, ROW_TILES)
             b, quarter = divmod(i, PACK)
-            rows = z_rows[b][:, 0 : PACK * widths[c]].rearrange("m (u j p e) -> m u j p e", u=2, p=P, e=2)
+            rows = pass_rows(c, b).rearrange("m (u j p e) -> m u j p e", u=2, p=P, e=2)
             sums = sum_banks[turn % len(sum_banks)][:, 0 : widths[c]]
             nc.scalar.copy(
                 out=rows[:, :, :, 32 * quarter : 32 * (quarter + 1), :],
@@ -256,7 +260,7 @@ def tile_list_hive_diary_kernel(
 
         def quantise_z(c, b):
             blocks = widths[c] // P
-            pairs = z_rows[b][:, 0 : PACK * widths[c]].bitcast(F32)
+            pairs = pass_rows(c, b).bitcast(F32)
             for j0 in range(0, blocks, 2):
                 g = (CHUNKS[c][0] + j0 * P) // GROUP
                 grouped = stage.tile([P, GROUP * PACK], BF16, name="z_grouped", tag="z_grouped", bufs=3, align_bytes=64)
@@ -291,7 +295,7 @@ def tile_list_hive_diary_kernel(
                         stop=(b == PASSES - 1),
                     )
 
-        held_back = list(range(1, SQUARED_UNITS))
+        held_back = [1, 2]
 
         def score_steps(unit, g, tiles, den, num):
             cols = slice(0, len(tiles) * GROUP)
@@ -299,8 +303,10 @@ def tile_list_hive_diary_kernel(
             size = casts[unit % 2][:, cols]
             root = rooms[1][:, slot : slot + BANK][:, cols]
             part = rooms[3][:, slot : slot + BANK][:, cols]
-            squared = unit < SQUARED_UNITS or unit == 8
-            num_step = 3 if unit in held_back else 2
+            if unit in (4, 5):
+                part = z_rows[PASSES - 1][:].bitcast(F32)[:, (unit - 4) * BANK : (unit - 3) * BANK]
+            squared = unit in SQUARED_UNITS
+            num_step = 3 if unit == held_back[1] else 2
 
             def absolute():
                 bank_sums(den_operand, g, tiles, den)
@@ -320,7 +326,10 @@ def tile_list_hive_diary_kernel(
             def last_product():
                 if num_step == 3:
                     bank_sums(num_operand, g, tiles, num)
-                result = stage.tile([P, BANK], F32, name="result", tag="result", bufs=RESULT_BUFS)
+                if unit == held_back[0]:
+                    result = weights[1][ROW_TILES - 1]
+                else:
+                    result = stage.tile([P, BANK], F32, name="result", tag="result", bufs=RESULT_BUFS)
                 nc.vector.tensor_tensor(result[:, cols], num[:, cols] if squared else root, part, MULT)
                 rows = out[tiles[0] * P : (tiles[-1] + 1) * P, g * GROUP : (g + 1) * GROUP]
                 nc.sync.dma_start(
@@ -333,10 +342,10 @@ def tile_list_hive_diary_kernel(
         units = []
         for unit in range(2 * (groups - 1)):
             g, pair = divmod(unit, 2)
-            num = sum_banks[held_back.index(unit)] if unit in held_back else num_banks[unit % 2]
+            num = [waiting_bank, sum_banks[0]][held_back.index(unit)] if unit in held_back else num_banks[unit % 2]
             units.append((g, [2 * pair, 2 * pair + 1], den_banks[unit % 2], num))
-        last_dens = [sum_banks[2], den_banks[0], den_banks[1], sum_banks[2]]
-        last_nums = [word_bank, sum_banks[0], sum_banks[1], num_banks[0]]
+        last_dens = [sum_banks[1], den_banks[0], den_banks[1], sum_banks[1]]
+        last_nums = [word_bank, waiting_bank, sum_banks[0], num_banks[0]]
         for tile in range(N // P):
             units.append((groups - 1, [tile], last_dens[tile], last_nums[tile]))
         steps = [score_steps(unit, *what) for unit, what in enumerate(units)]
@@ -356,8 +365,9 @@ def tile_list_hive_diary_kernel(
                 if i % PACK == PACK - 1:
                     quantise_z(c, i // PACK)
             if FIRST_SCORE_TURN <= turn < turns:
-                for step in queue[0 : STEPS[turn % 2]]:
+                count = STEPS[turn % 2] if turn < turns - 1 else 1
+                for step in queue[0:count]:
                     step()
-                queue = queue[STEPS[turn % 2] :]
+                queue = queue[count:]
         for step in [steps[unit][3] for unit in held_back] + queue:
             step()

@@ -125,16 +125,16 @@ def tile_list_hive_diary_kernel(
         nc.gpsimd.memset(one[:], 1.0)
         warm = held("warm", [P, 1], F32)
         nc.scalar.activation(out=warm[:], in_=one[:], func=ACT.Abs_reciprocal_sqrt, bias=1.0)
+        load_words(0)
         nc.sync.dma_start(tab_list[:], offs)
-        nc.sync.dma_start(put_list[:], offs2)
         for q in range(QUADRANTS):
             nc.sync.dma_start(
                 out=planes[32 * q : 32 * q + 4 * PASSES, :].bitcast(I32),
                 in_=tab_scales[:, 4 * q : 4 * q + 4, :].bitcast(I32),
             )
-        load_words(0)
         w1_raw = [load_weight(w1, 0, P, rooms[0])]
         load_words(1)
+        nc.sync.dma_start(put_list[:], offs2)
         nc.sync.dma_start(out=wgs_sb[:, 0:FIRST], in_=wgs[:, 0:FIRST])
         load_page(0)
         second_raw = load_weight(w1, P, P, second_room)
@@ -162,8 +162,8 @@ def tile_list_hive_diary_kernel(
         def pick(picked, table, first, end):
             nc.vector.tensor_copy(picked[:, first:end], table[:].indirect(entries(tab_list, first, end)))
 
-        pick(picked_planes, planes, 0, S)
         pick(picked_words[0], words[0], 0, S)
+        pick(picked_planes, planes, 0, S)
         pick(picked_words[1], words[1], 0, FIRST)
         w1_mx = quantise_weight("w1_0", w1_raw[0], casts[0])
         pick(picked_words[1], words[1], FIRST, S)

@@ -36,7 +36,7 @@ CHUNKS = [(0, 512), (512, 768), (768, 1024)]
 RING = 3
 FIRST_SCORE_TURN = 12
 STEPS = (1, 2)
-SQUARED_UNITS = (0, 1, 2, 4, 5, 8)
+SQUARED_UNITS = (0, 1, 2, 3, 4, 5, 8)
 RESULT_BUFS = 6
 
 
@@ -147,10 +147,10 @@ def tile_list_hive_diary_kernel(
         nc.sync.dma_start(out=w2_codes[:].bitcast(I32), in_=w2_words.rearrange("a p c -> p a c").bitcast(I32))
         nc.sync.dma_start(before_list[:], offs3)
         nc.sync.dma_start(after_list[:], offs4)
-        nc.gpsimd.memset(lam_rows[:], 0.0)
-        nc.sync.dma_start(out=lam_rows[0:ROW_TILES, :], in_=lam.rearrange("(i p) -> i p", p=P))
         load_page(6)
         load_page(7)
+        nc.gpsimd.memset(lam_rows[:], 0.0)
+        nc.sync.dma_start(out=lam_rows[0:ROW_TILES, :], in_=lam.rearrange("(i p) -> i p", p=P))
         nc.gpsimd.memset(w2_planes[:].bitcast(I32), 0)
         for q in range(QUADRANTS):
             nc.sync.dma_start(
@@ -222,16 +222,19 @@ def tile_list_hive_diary_kernel(
         z_rows = [held(f"z_rows{b}", [P, PACK * BANK], BF16) for b in range(PASSES)]
         z_codes = [[held(f"z_codes{g}_{b}", [P, GROUP], U32) for b in range(PASSES)] for g in range(groups)]
         z_scales = [[held(f"z_scales{g}_{b}", [P, GROUP], U8) for b in range(PASSES)] for g in range(groups)]
-        visits = [h_bufs[ROW_TILES - 1], wgs_sb]
+        visits = [h_bufs[ROW_TILES - 2], wgs_sb]
 
-        def fetch(turn):
+        def sum_bank(turn, lo):
+            return word_bank if lo > 0 else sum_banks[turn % len(sum_banks)]
+
+        def fetch(turn, lo, width):
             c, i = divmod(turn, ROW_TILES)
-            width = widths[c]
-            piece, which = divmod(turn % min(RING, S // width), 2)
-            weighed = visits[which][:, piece * 2 * width : (piece + 1) * 2 * width]
-            bank = sum_banks[turn % len(sum_banks)]
+            piece, which = divmod(turn % min(RING, S // widths[c]), 2)
+            first = piece * 2 * widths[c] + 2 * lo
+            weighed = visits[which][:, first : first + 2 * width]
+            bank = sum_bank(turn, lo)
             for n, days in enumerate((before_list, after_list)):
-                visit = pages[i][:].indirect(entries(days, *CHUNKS[c]))
+                visit = pages[i][:].indirect(entries(days, CHUNKS[c][0] + lo, CHUNKS[c][0] + lo + width))
                 nc.vector.tensor_tensor(weighed[:, n * width : (n + 1) * width], visit, weights[n][i][:, 0:width], MULT)
             for j in range(width // P):
                 for n in (1, 0):
@@ -248,31 +251,27 @@ def tile_list_hive_diary_kernel(
             first = 0 if widths[c] == BANK else P
             return z_rows[b][:, first : first + PACK * widths[c]]
 
-        def collect(turn):
+        def collect(turn, lo, width):
             c, i = divmod(turn, ROW_TILES)
             b, quarter = divmod(i, PACK)
-            rows = pass_rows(c, b).rearrange("m (u j p e) -> m u j p e", u=2, p=P, e=2)
-            sums = sum_banks[turn % len(sum_banks)][:, 0 : widths[c]]
+            rows = pass_rows(c, b).rearrange("m (j u p e) -> m j u p e", u=2, p=P, e=2)
             nc.scalar.copy(
-                out=rows[:, :, :, 32 * quarter : 32 * (quarter + 1), :],
-                in_=sums.rearrange("m (j p u e) -> m u j p e", p=32, u=2, e=2),
+                out=rows[:, lo // P : (lo + width) // P, :, 32 * quarter : 32 * (quarter + 1), :],
+                in_=sum_bank(turn, lo)[:, 0:width].rearrange("m (j p u e) -> m j u p e", p=32, u=2, e=2),
             )
 
-        def quantise_z(c, b):
-            blocks = widths[c] // P
-            pairs = pass_rows(c, b).bitcast(F32)
-            for j0 in range(0, blocks, 2):
-                g = (CHUNKS[c][0] + j0 * P) // GROUP
-                grouped = stage.tile([P, GROUP * PACK], BF16, name="z_grouped", tag="z_grouped", bufs=3, align_bytes=64)
-                for j in range(2):
-                    for u in range(2):
-                        source, target = (u * blocks + j0 + j) * P, (2 * j + u) * P
-                        nc.tensor.transpose(word_bank[:, target : target + P], pairs[:, source : source + P], ident[:])
-                nc.scalar.copy(
-                    out=grouped[:].bitcast(F32).rearrange("p (j m u) -> p j m u", j=2, u=2),
-                    in_=word_bank[:].rearrange("p (j u m) -> p j m u", j=2, u=2),
-                )
-                nc.vector.quantize_mx(out=z_codes[g][b][:].bitcast(FP8X4), scales=z_scales[g][b][:], in_=grouped[:])
+        def quantise_z(c, b, lo, width, bank):
+            g, first = divmod(CHUNKS[c][0] + lo, GROUP)
+            pairs = pass_rows(c, b).bitcast(F32)[:, 2 * lo : 2 * (lo + width)]
+            grouped = stage.tile([P, width * PACK], BF16, name="z_grouped", tag="z_grouped", bufs=3, align_bytes=64)
+            for n in range(2 * width // P):
+                nc.tensor.transpose(bank[:, n * P : (n + 1) * P], pairs[:, n * P : (n + 1) * P], ident[:])
+            nc.scalar.copy(
+                out=grouped[:].bitcast(F32).rearrange("p (j m u) -> p j m u", m=P, u=2),
+                in_=bank[:, 0 : 2 * width].rearrange("p (j u m) -> p j m u", m=P, u=2),
+            )
+            cols = slice(first, first + width)
+            nc.vector.quantize_mx(out=z_codes[g][b][:, cols].bitcast(FP8X4), scales=z_scales[g][b][:, cols], in_=grouped[:])
 
         def den_operand(tile, b):
             return stationary(w3_mx, tile, b)
@@ -327,7 +326,7 @@ def tile_list_hive_diary_kernel(
                 if num_step == 3:
                     bank_sums(num_operand, g, tiles, num)
                 if unit == held_back[0]:
-                    result = weights[1][ROW_TILES - 1]
+                    result = weights[0][ROW_TILES - 1]
                 else:
                     result = stage.tile([P, BANK], F32, name="result", tag="result", bufs=RESULT_BUFS)
                 nc.vector.tensor_tensor(result[:, cols], num[:, cols] if squared else root, part, MULT)
@@ -356,18 +355,24 @@ def tile_list_hive_diary_kernel(
             if 0 <= n - k < len(units) and not (k == 3 and n - k in held_back)
         ]
 
-        for turn in range(turns + 1):
-            if turn < turns:
-                fetch(turn)
+        last = turns - 1
+        for turn in range(turns):
+            fetch(turn, 0, widths[turn // ROW_TILES] if turn < last else P)
             if turn >= 1:
-                collect(turn - 1)
                 c, i = divmod(turn - 1, ROW_TILES)
+                collect(turn - 1, 0, widths[c])
                 if i % PACK == PACK - 1:
-                    quantise_z(c, i // PACK)
-            if FIRST_SCORE_TURN <= turn < turns:
-                count = STEPS[turn % 2] if turn < turns - 1 else 1
+                    for lo in range(0, widths[c], GROUP):
+                        quantise_z(c, i // PACK, lo, GROUP, word_bank)
+            if FIRST_SCORE_TURN <= turn:
+                count = STEPS[turn % 2] if turn < last else 1
                 for step in queue[0:count]:
                     step()
                 queue = queue[count:]
+        fetch(last, P, P)
+        for lo in (0, P):
+            collect(last, lo, P)
+        for lo in (0, P):
+            quantise_z(len(CHUNKS) - 1, PASSES - 1, lo, P, sum_bank(last, lo))
         for step in [steps[unit][3] for unit in held_back] + queue:
             step()

@@ -34,8 +34,10 @@ SCORE_SLOTS = 4
 
 CHUNKS = [(0, 512), (512, 768), (768, 1024)]
 RING = 3
-FIRST_SCORE_TURN = 12
-STEPS = (1, 2)
+PACE = {
+    12: [(0, 0)], 13: [(0, 1), (1, 0)], 14: [(0, 2)], 15: [(1, 1), (2, 0)], 16: [(1, 2)], 17: [(2, 1), (3, 0)],
+    18: [(2, 2)], 19: [(3, 1), (4, 0)], 20: [(3, 2)], 21: [(4, 1), (5, 0)],
+}
 SQUARED_UNITS = (0, 1, 2, 3, 4, 5, 8)
 RESULT_BUFS = 6
 
@@ -66,7 +68,10 @@ def tile_list_hive_diary_kernel(
         wgs_sb = held("wgs_sb", [P, S], F32)
         lam_rows = held("lam_rows", [P, P], F32)
         lam_cols = held("lam_cols", [P, ROW_TILES], F32)
-        weights = [[held(f"weight{n}_{i}", [P, BANK], F32) for i in range(ROW_TILES)] for n in range(2)]
+        weights = [[held(f"weight{n}_{i}", [P, BANK], F32)[:] for i in range(ROW_TILES - 1)] for n in range(2)]
+        last_weights = [held(f"last_weight{n}", [P, GROUP + S], F32) for n in range(2)]
+        for n in range(2):
+            weights[n].append(last_weights[n][:, 0:BANK])
         one = held("one", [P, 1], F32)
         ident = held("ident", [P, P], F32)
         w2_codes = held("w2_codes", [P, PASSES, 2 * N], U8)
@@ -105,7 +110,7 @@ def tile_list_hive_diary_kernel(
         def quantise_weight(name, raws, cast):
             width = raws[0].shape[2]
             size = PACK * width
-            grouped = cast[:].bitcast(BF16)[:, 0 : PASSES * size]
+            grouped = cast.bitcast(BF16)[:, 0 : PASSES * size]
             for a in range(PASSES):
                 nc.scalar.copy(
                     out=grouped[:, a * size : (a + 1) * size].rearrange("p (c i j) -> p c j i", i=4, j=PACK),
@@ -165,9 +170,9 @@ def tile_list_hive_diary_kernel(
         pick(picked_words[0], words[0], 0, S)
         pick(picked_planes, planes, 0, S)
         pick(picked_words[1], words[1], 0, FIRST)
-        w1_mx = quantise_weight("w1_0", w1_raw[0], casts[0])
+        w1_mx = quantise_weight("w1_0", w1_raw[0], casts[0][:])
         pick(picked_words[1], words[1], FIRST, S)
-        w1_mx = w1_mx + quantise_weight("w1_second", second_raw, second_cast)
+        w1_mx = w1_mx + quantise_weight("w1_second", second_raw, second_cast[:])
 
         def write_entries(i):
             if i == 0:
@@ -199,23 +204,22 @@ def tile_list_hive_diary_kernel(
                 days = pages[i][:].indirect(entries(put_list, first, end))
                 nc.vector.tensor_tensor(days, h, wgs_sb[:, first:end], MULT)
 
-        w3_mx = []
+        w3_raw, w3_mx = [], []
         for i in range(ROW_TILES):
             if i % 2 == 1 and i + 1 < ROW_TILES:
                 c = (i + 1) // 2
-                w1_mx = w1_mx + quantise_weight(f"w1_{c}", w1_raw[c], casts[c % 2])
+                w1_mx = w1_mx + quantise_weight(f"w1_{c}", w1_raw[c], casts[c % 2][:])
             write_entries(i)
             if i in (4, 5):
                 c = i - 4
-                raws = load_weight(w3, c * W_COLS, W_COLS, rooms[1 + 2 * c])
-                w3_mx = w3_mx + quantise_weight(f"w3_{c}", raws, casts[c])
+                w3_raw.append(load_weight(w3, c * W_COLS, W_COLS, rooms[1 + 2 * c]))
 
         nc.tensor.transpose(h_banks[1][:, 0:P], lam_rows[:], ident[:])
         nc.scalar.copy(out=lam_cols[:], in_=h_banks[1][:, 0:ROW_TILES])
         for i in range(ROW_TILES):
             spread = lam_cols[:, i : i + 1].to_broadcast([P, BANK])
-            nc.scalar.activation(out=weights[0][i][:], in_=spread, func=ACT.Copy, scale=-1.0, bias=1.0)
-            nc.scalar.copy(out=weights[1][i][:], in_=spread)
+            nc.scalar.activation(out=weights[0][i], in_=spread, func=ACT.Copy, scale=-1.0, bias=1.0)
+            nc.scalar.copy(out=weights[1][i], in_=spread)
 
         widths = [end - first for first, end in CHUNKS]
         turns, groups = len(CHUNKS) * ROW_TILES, TREATMENTS // GROUP
@@ -294,7 +298,7 @@ def tile_list_hive_diary_kernel(
                         stop=(b == PASSES - 1),
                     )
 
-        held_back = [1, 2]
+        held_back = [1, 0, 3, 2]
 
         def score_steps(unit, g, tiles, den, num):
             cols = slice(0, len(tiles) * GROUP)
@@ -305,7 +309,7 @@ def tile_list_hive_diary_kernel(
             if unit in (4, 5):
                 part = z_rows[PASSES - 1][:].bitcast(F32)[:, (unit - 4) * BANK : (unit - 3) * BANK]
             squared = unit in SQUARED_UNITS
-            num_step = 3 if unit == held_back[1] else 2
+            num_step = 3 if unit == 2 else 2
 
             def absolute():
                 bank_sums(den_operand, g, tiles, den)
@@ -325,8 +329,8 @@ def tile_list_hive_diary_kernel(
             def last_product():
                 if num_step == 3:
                     bank_sums(num_operand, g, tiles, num)
-                if unit == held_back[0]:
-                    result = weights[0][ROW_TILES - 1]
+                if unit in (0, 1, 3):
+                    result = {1: weights[0][-1], 0: weights[1][-1], 3: visits[0][:, BANK : 2 * BANK]}[unit]
                 else:
                     result = stage.tile([P, BANK], F32, name="result", tag="result", bufs=RESULT_BUFS)
                 nc.vector.tensor_tensor(result[:, cols], num[:, cols] if squared else root, part, MULT)
@@ -341,10 +345,10 @@ def tile_list_hive_diary_kernel(
         units = []
         for unit in range(2 * (groups - 1)):
             g, pair = divmod(unit, 2)
-            num = [waiting_bank, sum_banks[0]][held_back.index(unit)] if unit in held_back else num_banks[unit % 2]
+            num = [num_banks[0], waiting_bank, sum_banks[0], num_banks[1], den_banks[0], den_banks[1]][unit]
             units.append((g, [2 * pair, 2 * pair + 1], den_banks[unit % 2], num))
-        last_dens = [sum_banks[1], den_banks[0], den_banks[1], sum_banks[1]]
-        last_nums = [word_bank, waiting_bank, sum_banks[0], num_banks[0]]
+        last_dens = [sum_banks[1], waiting_bank, num_banks[0], sum_banks[1]]
+        last_nums = [word_bank, num_banks[1], sum_banks[0], den_banks[0]]
         for tile in range(N // P):
             units.append((groups - 1, [tile], last_dens[tile], last_nums[tile]))
         steps = [score_steps(unit, *what) for unit, what in enumerate(units)]
@@ -364,11 +368,12 @@ def tile_list_hive_diary_kernel(
                 if i % PACK == PACK - 1:
                     for lo in range(0, widths[c], GROUP):
                         quantise_z(c, i // PACK, lo, GROUP, word_bank)
-            if FIRST_SCORE_TURN <= turn:
-                count = STEPS[turn % 2] if turn < last else 1
-                for step in queue[0:count]:
-                    step()
-                queue = queue[count:]
+            if turn == ROW_TILES - 1:
+                for c in range(2):
+                    w3_mx.extend(quantise_weight(f"w3_{c}", w3_raw[c], last_weights[c][:, GROUP : GROUP + S]))
+            for unit, k in PACE.get(turn, []):
+                steps[unit][k]()
+                queue.remove(steps[unit][k])
         fetch(last, P, P)
         for lo in (0, P):
             collect(last, lo, P)

from contextlib import ExitStack

import concourse.mybir as mybir
from concourse.masks import make_identity

K, H, N, T, S, T2, TREATMENTS = 1024, 1024, 512, 2048, 1024, 2048, 1024
FLOPS = 2 * K * H * S + 2 * 2 * H * N * TREATMENTS

F32 = mybir.dt.float32
BF16 = mybir.dt.bfloat16
I32 = mybir.dt.int32
U32 = mybir.dt.uint32
U16 = mybir.dt.uint16
U8 = mybir.dt.uint8
FP8X4 = mybir.dt.float8_e4m3fn_x4
FP4X4 = mybir.dt.float4_e2m1fn_x4
ACT = mybir.ActivationFunctionType
MULT = mybir.AluOpType.mult

P = 128
PACK = 4
K_PASS = P * PACK
PASSES = 2
BANK = 512
QUADRANTS = 4
LIST_ROWS = 16
ROW_TILES = H // P
QUARTER = S // 4
FIRST = 384
HALF = S // 2
W_COLS = 256
GROUP = 2 * P
SCORE_SLOTS = 4

CHUNKS = [(0, 512), (512, 768), (768, 1024)]
RING = 3
PACE = {
    12: [(0, 0)], 13: [(0, 1), (1, 0)], 14: [(0, 2)], 15: [(1, 1), (2, 0)], 16: [(1, 2)], 17: [(2, 1), (3, 0)],
    18: [(2, 2)], 19: [(3, 1), (4, 0)], 20: [(3, 2)], 21: [(4, 1), (5, 0)],
}
SQUARED_UNITS = (0, 1, 2, 3, 4, 5, 8)
RESULT_BUFS = 6


def tile_list_hive_diary_kernel(
    tc, tab_words, tab_scales, offs, w1, wgs, page0, offs2, offs3, offs4, lam, w2_words, w2_scales, w3, out
):
    nc = tc.nc
    with ExitStack() as ctx:
        keep = ctx.enter_context(tc.tile_pool(name="keep", bufs=1))
        stage = ctx.enter_context(tc.tile_pool(name="stage", bufs=2))
        psum = ctx.enter_context(tc.psum_pool(name="psum", bufs=1))

        def held(name, shape, dtype):
            return keep.tile(shape, dtype, name=name, align_bytes=64)

        def entries(offsets, first, end):
            return offsets[:, first // LIST_ROWS : end // LIST_ROWS]

        tab_list, put_list, before_list, after_list = [
            keep.tile([P, S // LIST_ROWS], U16, name=f"list{n}") for n in range(4)
        ]
        words = [held(f"words{a}", [P, T], U32) for a in range(PASSES)]
        planes = held("planes", [P, T], U8)
        picked_words = [held(f"picked_words{a}", [P, S], U32) for a in range(PASSES)]
        picked_planes = held("picked_planes", [P, S], U8)
        pages = [held(f"page{i}", [P, T2], F32) for i in range(ROW_TILES)]
        wgs_sb = held("wgs_sb", [P, S], F32)
        lam_rows = held("lam_rows", [P, P], F32)
        lam_cols = held("lam_cols", [P, ROW_TILES], F32)
        weights = [[held(f"weight{n}_{i}", [P, BANK], F32)[:] for i in range(ROW_TILES - 1)] for n in range(2)]
        last_weights = [held(f"last_weight{n}", [P, GROUP + S], F32) for n in range(2)]
        for n in range(2):
            weights[n].append(last_weights[n][:, 0:BANK])
        one = held("one", [P, 1], F32)
        ident = held("ident", [P, P], F32)
        w2_codes = held("w2_codes", [P, PASSES, 2 * N], U8)
        w2_planes = held("w2_planes", [P, PASSES, N], U8)

        rooms = [held(f"room{c}", [P, PASSES * PACK * W_COLS], F32) for c in range(H // W_COLS)]
        casts = [held(f"cast{n}", [P, S], F32) for n in range(2)]
        second_space, second_cast = held("second_space", [P, HALF + S], F32), held("second_cast", [P, HALF], F32)
        second_room = second_space[:, HALF : HALF + S]
        low, high = slice(0, S), slice(S, 2 * S)
        h_bufs = {
            i: rooms[(i + 1) // 2 % len(rooms)][:, high] if i % 2 == 1 else rooms[i // 2 - 1][:, low]
            for i in range(1, ROW_TILES)
        }

        banks = [psum.tile([P, BANK], F32, name=f"bank{b}") for b in range(8)]
        h_banks = banks[0:2]
        sum_banks, word_bank, waiting_bank = banks[2:4], banks[4], banks[1]
        den_banks, num_banks = banks[5:7], [banks[7], banks[0]]

        def load_words(a):
            source = tab_words[a].rearrange("p t i -> p (t i)").bitcast(I32)
            nc.sync.dma_start(out=words[a][:].bitcast(I32), in_=source)

        def load_page(i):
            nc.sync.dma_start(out=pages[i][:], in_=page0[i * P : (i + 1) * P, :])

        def load_weight(w, first, width, room):
            size = PACK * width
            raws = [room[:, a * size : (a + 1) * size].rearrange("p (j c) -> p j c", j=PACK) for a in range(PASSES)]
            for a in range(PASSES):
                rows = w[a * K_PASS : (a + 1) * K_PASS, first : first + width]
                nc.sync.dma_start(out=raws[a], in_=rows.rearrange("(p j) c -> p j c", j=PACK))
            return raws

        def quantise_weight(name, raws, cast):
            width = raws[0].shape[2]
            size = PACK * width
            grouped = cast.bitcast(BF16)[:, 0 : PASSES * size]
            for a in range(PASSES):
                nc.scalar.copy(
                    out=grouped[:, a * size : (a + 1) * size].rearrange("p (c i j) -> p c j i", i=4, j=PACK),
                    in_=raws[a].rearrange("p j (c i) -> p c j i", i=4),
                )
            codes = held(f"{name}_codes", [P, PASSES * width], U32)
            scales = held(f"{name}_scales", [P, PASSES * width], U8)
            nc.vector.quantize_mx(out=codes[:].bitcast(FP8X4), scales=scales[:], in_=grouped)
            return [(codes, scales, width, first) for first in range(0, width, P)]

        def stationary(weight_mx, tile, a):
            codes, scales, width, first = weight_mx[tile]
            first = a * width + first
            return codes[:, first : first + P].bitcast(FP8X4), scales[:, first : first + P]

        nc.gpsimd.memset(planes[:].bitcast(I32), 0)
        nc.gpsimd.memset(one[:], 1.0)
        warm = held("warm", [P, 1], F32)
        nc.scalar.activation(out=warm[:], in_=one[:], func=ACT.Abs_reciprocal_sqrt, bias=1.0)
        load_words(0)
        nc.sync.dma_start(tab_list[:], offs)
        for q in range(QUADRANTS):
            nc.sync.dma_start(
                out=planes[32 * q : 32 * q + 4 * PASSES, :].bitcast(I32),
                in_=tab_scales[:, 4 * q : 4 * q + 4, :].bitcast(I32),
            )
        w1_raw = [load_weight(w1, 0, P, rooms[0])]
        load_words(1)
        nc.sync.dma_start(put_list[:], offs2)
        nc.sync.dma_start(out=wgs_sb[:, 0:FIRST], in_=wgs[:, 0:FIRST])
        load_page(0)
        second_raw = load_weight(w1, P, P, second_room)
        nc.sync.dma_start(out=wgs_sb[:, FIRST:S], in_=wgs[:, FIRST:S])
        for c in range(1, len(rooms)):
            w1_raw.append(load_weight(w1, c * W_COLS, W_COLS, rooms[c]))
            load_page(c)
        load_page(4)
        load_page(5)
        nc.sync.dma_start(out=w2_codes[:].bitcast(I32), in_=w2_words.rearrange("a p c -> p a c").bitcast(I32))
        nc.sync.dma_start(before_list[:], offs3)
        nc.sync.dma_start(after_list[:], offs4)
        load_page(6)
        load_page(7)
        nc.gpsimd.memset(lam_rows[:], 0.0)
        nc.sync.dma_start(out=lam_rows[0:ROW_TILES, :], in_=lam.rearrange("(i p) -> i p", p=P))
        nc.gpsimd.memset(w2_planes[:].bitcast(I32), 0)
        for q in range(QUADRANTS):
            nc.sync.dma_start(
                out=w2_planes[32 * q : 32 * q + 4, :, :].bitcast(I32),
                in_=w2_scales[:, 4 * q : 4 * q + 4, :].rearrange("a r c -> r a c").bitcast(I32),
            )
        make_identity(nc, ident[:])

        def pick(picked, table, first, end):
            nc.vector.tensor_copy(picked[:, first:end], table[:].indirect(entries(tab_list, first, end)))

        pick(picked_words[0], words[0], 0, S)
        pick(picked_planes, planes, 0, S)
        pick(picked_words[1], words[1], 0, FIRST)
        w1_mx = quantise_weight("w1_0", w1_raw[0], casts[0][:])
        pick(picked_words[1], words[1], FIRST, S)
        w1_mx = w1_mx + quantise_weight("w1_second", second_raw, second_cast[:])

        def write_entries(i):
            if i == 0:
                first, rest = casts[1][:, HALF : HALF + FIRST], second_space[:, 0 : S - FIRST]
                sums = [(0, QUARTER, banks[0]), (QUARTER, FIRST, banks[2]), (FIRST, HALF, banks[3]), (HALF, S, banks[1])]
                copies = [[(first[:, 0:QUARTER], 0, QUARTER)], [(first[:, QUARTER:FIRST], QUARTER, FIRST)]]
                copies.append([(rest[:, 0 : HALF - FIRST], FIRST, HALF)])
                copies.append([(rest[:, HALF - FIRST : HALF], HALF, HALF + FIRST), (rest[:, HALF : S - FIRST], HALF + FIRST, S)])
                pieces = [(first, 0, FIRST), (rest, FIRST, S)]
            else:
                sums = [(hf * HALF, (hf + 1) * HALF, h_banks[hf]) for hf in range(2)]
                copies = [[(h_bufs[i][:, lo:hi], lo, hi)] for lo, hi, bank in sums]
                pieces = [(h_bufs[i], 0, S)]
            for (lo, hi, bank), targets in zip(sums, copies):
                for a in range(PASSES):
                    codes, scales = stationary(w1_mx, i, a)
                    nc.tensor.matmul_mx(
                        out=bank[:, 0 : hi - lo],
                        lhsT=codes,
                        lhsT_scale=scales,
                        rhs=picked_words[a][:, lo:hi].bitcast(FP8X4),
                        rhs_scale=picked_planes[4 * a : P, lo:hi],
                        start=(a == 0),
                        stop=(a == PASSES - 1),
                    )
                for target, first, end in targets:
                    nc.scalar.copy(out=target, in_=bank[:, first - lo : end - lo])
            for h, first, end in pieces:
                days = pages[i][:].indirect(entries(put_list, first, end))
                nc.vector.tensor_tensor(days, h, wgs_sb[:, first:end], MULT)

        w3_raw, w3_mx = [], []
        for i in range(ROW_TILES):
            if i % 2 == 1 and i + 1 < ROW_TILES:
                c = (i + 1) // 2
                w1_mx = w1_mx + quantise_weight(f"w1_{c}", w1_raw[c], casts[c % 2][:])
            write_entries(i)
            if i in (4, 5):
                c = i - 4
                w3_raw.append(load_weight(w3, c * W_COLS, W_COLS, rooms[1 + 2 * c]))

        nc.tensor.transpose(h_banks[1][:, 0:P], lam_rows[:], ident[:])
        nc.scalar.copy(out=lam_cols[:], in_=h_banks[1][:, 0:ROW_TILES])
        for i in range(ROW_TILES):
            spread = lam_cols[:, i : i + 1].to_broadcast([P, BANK])
            nc.scalar.activation(out=weights[0][i], in_=spread, func=ACT.Copy, scale=-1.0, bias=1.0)
            nc.scalar.copy(out=weights[1][i], in_=spread)

        widths = [end - first for first, end in CHUNKS]
        turns, groups = len(CHUNKS) * ROW_TILES, TREATMENTS // GROUP
        z_rows = [held(f"z_rows{b}", [P, PACK * BANK], BF16) for b in range(PASSES)]
        z_codes = [[held(f"z_codes{g}_{b}", [P, GROUP], U32) for b in range(PASSES)] for g in range(groups)]
        z_scales = [[held(f"z_scales{g}_{b}", [P, GROUP], U8) for b in range(PASSES)] for g in range(groups)]
        visits = [h_bufs[ROW_TILES - 2], wgs_sb]

        def sum_bank(turn, lo):
            return word_bank if lo > 0 else sum_banks[turn % len(sum_banks)]

        def fetch(turn, lo, width):
            c, i = divmod(turn, ROW_TILES)
            piece, which = divmod(turn % min(RING, S // widths[c]), 2)
            first = piece * 2 * widths[c] + 2 * lo
            weighed = visits[which][:, first : first + 2 * width]
            bank = sum_bank(turn, lo)
            for n, days in enumerate((before_list, after_list)):
                visit = pages[i][:].indirect(entries(days, CHUNKS[c][0] + lo, CHUNKS[c][0] + lo + width))
                nc.vector.tensor_tensor(weighed[:, n * width : (n + 1) * width], visit, weights[n][i][:, 0:width], MULT)
            for j in range(width // P):
                for n in (1, 0):
                    nc.tensor.matmul(
                        bank[:, j * P : (j + 1) * P],
                        weighed[:, n * width + j * P : n * width + (j + 1) * P],
                        ident[:],
                        is_transpose=True,
                        start=(n == 1),
                        stop=(n == 0),
                    )

        def pass_rows(c, b):
            first = 0 if widths[c] == BANK else P
            return z_rows[b][:, first : first + PACK * widths[c]]

        def collect(turn, lo, width):
            c, i = divmod(turn, ROW_TILES)
            b, quarter = divmod(i, PACK)
            rows = pass_rows(c, b).rearrange("m (j u p e) -> m j u p e", u=2, p=P, e=2)
            nc.scalar.copy(
                out=rows[:, lo // P : (lo + width) // P, :, 32 * quarter : 32 * (quarter + 1), :],
                in_=sum_bank(turn, lo)[:, 0:width].rearrange("m (j p u e) -> m j u p e", p=32, u=2, e=2),
            )

        def quantise_z(c, b, lo, width, bank):
            g, first = divmod(CHUNKS[c][0] + lo, GROUP)
            pairs = pass_rows(c, b).bitcast(F32)[:, 2 * lo : 2 * (lo + width)]
            grouped = stage.tile([P, width * PACK], BF16, name="z_grouped", tag="z_grouped", bufs=3, align_bytes=64)
            for n in range(2 * width // P):
                nc.tensor.transpose(bank[:, n * P : (n + 1) * P], pairs[:, n * P : (n + 1) * P], ident[:])
            nc.scalar.copy(
                out=grouped[:].bitcast(F32).rearrange("p (j m u) -> p j m u", m=P, u=2),
                in_=bank[:, 0 : 2 * width].rearrange("p (j u m) -> p j m u", m=P, u=2),
            )
            cols = slice(first, first + width)
            nc.vector.quantize_mx(out=z_codes[g][b][:, cols].bitcast(FP8X4), scales=z_scales[g][b][:, cols], in_=grouped[:])

        def den_operand(tile, b):
            return stationary(w3_mx, tile, b)

        def num_operand(tile, b):
            codes = w2_codes[:, b, 2 * tile * P : 2 * (tile + 1) * P].bitcast(FP4X4)
            return codes, w2_planes[:, b, tile * P : (tile + 1) * P]

        def bank_sums(operand, g, tiles, bank):
            for n, tile in enumerate(tiles):
                for b in range(PASSES):
                    codes, scales = operand(tile, b)
                    nc.tensor.matmul_mx(
                        out=bank[:, n * GROUP : (n + 1) * GROUP],
                        lhsT=codes,
                        lhsT_scale=scales,
                        rhs=z_codes[g][b][:].bitcast(FP8X4),
                        rhs_scale=z_scales[g][b][:],
                        start=(b == 0),
                        stop=(b == PASSES - 1),
                    )

        held_back = [1, 0, 3, 2]

        def score_steps(unit, g, tiles, den, num):
            cols = slice(0, len(tiles) * GROUP)
            slot = (unit % SCORE_SLOTS) * BANK
            size = casts[unit % 2][:, cols]
            root = rooms[1][:, slot : slot + BANK][:, cols]
            part = rooms[3][:, slot : slot + BANK][:, cols]
            if unit in (4, 5):
                part = z_rows[PASSES - 1][:].bitcast(F32)[:, (unit - 4) * BANK : (unit - 3) * BANK]
            squared = unit in SQUARED_UNITS
            num_step = 3 if unit == 2 else 2

            def absolute():
                bank_sums(den_operand, g, tiles, den)
                nc.scalar.activation(out=size, in_=den[:, cols], func=ACT.Abs)

            def inverse_root():
                nc.scalar.activation(out=root, in_=size, func=ACT.Abs_reciprocal_sqrt, bias=1.0)

            def first_product():
                if num_step == 2:
                    bank_sums(num_operand, g, tiles, num)
                if squared:
                    nc.scalar.activation(out=part, in_=root, func=ACT.Square)
                else:
                    nc.vector.tensor_tensor(part, num[:, cols], root, MULT)

            def last_product():
                if num_step == 3:
                    bank_sums(num_operand, g, tiles, num)
                if unit in (0, 1, 3):
                    result = {1: weights[0][-1], 0: weights[1][-1], 3: visits[0][:, BANK : 2 * BANK]}[unit]
                else:
                    result = stage.tile([P, BANK], F32, name="result", tag="result", bufs=RESULT_BUFS)
                nc.vector.tensor_tensor(result[:, cols], num[:, cols] if squared else root, part, MULT)
                rows = out[tiles[0] * P : (tiles[-1] + 1) * P, g * GROUP : (g + 1) * GROUP]
                nc.sync.dma_start(
                    out=rows.rearrange("(t p) m -> p t m", p=P),
                    in_=result[:, cols].rearrange("p (t m) -> p t m", t=len(tiles)),
                )

            return [absolute, inverse_root, first_product, last_product]

        units = []
        for unit in range(2 * (groups - 1)):
            g, pair = divmod(unit, 2)
            num = [num_banks[0], waiting_bank, sum_banks[0], num_banks[1], den_banks[0], den_banks[1]][unit]
            units.append((g, [2 * pair, 2 * pair + 1], den_banks[unit % 2], num))
        last_dens = [sum_banks[1], waiting_bank, num_banks[0], sum_banks[1]]
        last_nums = [word_bank, num_banks[1], sum_banks[0], den_banks[0]]
        for tile in range(N // P):
            units.append((groups - 1, [tile], last_dens[tile], last_nums[tile]))
        steps = [score_steps(unit, *what) for unit, what in enumerate(units)]
        queue = [
            steps[n - k][k]
            for n in range(len(units) + 3)
            for k in (3, 2, 1, 0)
            if 0 <= n - k < len(units) and not (k == 3 and n - k in held_back)
        ]

        last = turns - 1
        for turn in range(turns):
            fetch(turn, 0, widths[turn // ROW_TILES] if turn < last else P)
            if turn >= 1:
                c, i = divmod(turn - 1, ROW_TILES)
                collect(turn - 1, 0, widths[c])
                if i % PACK == PACK - 1:
                    for lo in range(0, widths[c], GROUP):
                        quantise_z(c, i // PACK, lo, GROUP, word_bank)
            if turn == ROW_TILES - 1:
                for c in range(2):
                    w3_mx.extend(quantise_weight(f"w3_{c}", w3_raw[c], last_weights[c][:, GROUP : GROUP + S]))
            for unit, k in PACE.get(turn, []):
                steps[unit][k]()
                queue.remove(steps[unit][k])
        fetch(last, P, P)
        for lo in (0, P):
            collect(last, lo, P)
        for lo in (0, P):
            quantise_z(len(CHUNKS) - 1, PASSES - 1, lo, P, sum_bank(last, lo))
        for step in [steps[unit][3] for unit in held_back] + queue:
            step()
